import numpy as np, ml_dtypes
CORES = [35,38,43,46]
N = 4
BF = ml_dtypes.bfloat16
def gentries(a):
    return np.ascontiguousarray(a.reshape(8, 16, -1).transpose(0, 2, 1)).reshape(8, -1)
def gtable(e):
    e = np.asarray(e); return np.ascontiguousarray(e.reshape(8, -1, 16).transpose(0, 2, 1)).reshape(128, -1).astype(np.int32)
V, G, CAP, D, SH, RO = 2048, 512, 128, 4, 3, 3
def parts(rng):
    t = rng.integers(2 ** 18, 2 ** 19, (N, 8, 16, 1))
    r = np.minimum((t * rng.random((N, 8, 1, V)) * rng.random((N, 8, 16, V))).astype(np.int64), t - 1)
    nb = rng.integers(0, V + (N - 1) * G, (N, 8, D * V)); snd = np.argsort(rng.random((N, 8, N - 1, V)), axis=-1)[..., :G]
    return t, r, nb, np.ascontiguousarray(snd)
def heat(rng, t, r, share):
    m = (rng.random((N, 8, 1, V)) < share) & (rng.random(r.shape) < rng.random((N, 8, 1, V)))
    return np.where(m, np.minimum(t + ((2 ** 20 - t) * rng.random(r.shape)).astype(np.int64), 2 ** 20 - 1), r)
def pack(t, r, nb, snd):
    return {"r0": np.ascontiguousarray(r.reshape(N, 128, V)).astype(np.int32), "th": np.ascontiguousarray(t.reshape(N, 128, 1)).astype(np.int32),
            "nb": np.stack([gtable(a) for a in nb]), "snd": np.stack([gtable(a.reshape(8, -1)) for a in snd])}
def setup_inputs(rng):
    t, r, nb, snd = parts(rng); share = rng.choice(np.array([0.05, 0.15, 0.3, 0.5]), (N, 8, 1, 1))
    return pack(t, heat(rng, t, r, share), nb, snd)
def setup_inputs_room(rng):
    t, r, nb, snd = parts(rng); h = V // 2
    for q in range(N):
        for g in range(8):
            o = rng.permutation(V); a, b = o[:h], o[h:]; i = rng.integers(0, 16, h); lo = t[q, g, i, 0]
            r[q, g, i, a] = np.where(rng.random(h) < 0.5, lo, np.minimum(lo + ((2 ** 20 - lo) * rng.random(h)).astype(np.int64), 2 ** 20 - 1))
            for d in range(N - 1):
                n = int(rng.choice(np.array([0, 1, CAP - 1, CAP, CAP + 1, G])))
                if q == 0 and d == 0: n = (CAP, CAP + 1, G, CAP - 1, 1, 0, CAP, CAP + 1)[g]
                snd[q, g, d] = rng.permutation(np.concatenate([rng.permutation(a)[:n], rng.permutation(b)[:G - n]]))
    return pack(t, r, nb, snd)
def setup_inputs_ties(rng):
    t, r, nb, snd = parts(rng)
    base = rng.choice(np.array([1, 4, 7, 1000, 2 ** 16 - 1, 2 ** 19, 2 ** 20 - 1]), (N, 8, 1, 1)); base[0, 0] = 1; base[0, 1] = 2 ** 19; base[1, 0] = 2 ** 20 - 1
    t = np.minimum(base + rng.integers(0, 3, (N, 8, 16, 1)), 2 ** 20)
    r = (t - 1) * rng.integers(0, 2, (N, 8, 16, V)); hit = rng.random((N, 8, 1, V)) < 0.2
    r = np.where(hit, np.minimum(t - 1 + rng.integers(0, 3, r.shape), 2 ** 20 - 1), r)
    m = rng.permutation(V)[None, :]
    r[0, 0] = np.where(m < 3 * V // 10, t[0, 0], np.where(m < 6 * V // 10, rng.integers(2 ** 19, 2 ** 20, (16, V)), t[0, 0] - 1))
    return pack(t, r, nb, snd)
def setup_inputs_alike(rng):
    t, r, nb, snd = parts(rng); r = heat(rng, t, r, 0.2); r[..., 0] = 2 ** 20 - 1; r[..., V - 1] = 2 ** 20 - 1
    snd[:, ::2] = rng.choice(np.array([0, V - 1, V // 2, 3]), (N, 4, N - 1, G))
    nb[:, 1::2] = np.tile(nb[:, 1::2, :V], (1, 1, D))
    nb[:, 2] = rng.integers(V, V + (N - 1) * G, (N, D * V)); nb[:, 4] = rng.integers(0, V, (N, D * V))
    nb[:, 6] = rng.choice(np.array([0, V - 1, V, V + (N - 1) * G - 1]), (N, D * V))
    return pack(t, r, nb, snd)
def setup_inputs_cold(rng):
    t, r, nb, snd = parts(rng); share = rng.choice(np.array([0.1, 0.25, 0.4]), (N, 8, 1, 1))
    q = rng.permutation(N); share[q[0]] = 1.0; share[q[1]] = 0.0; share[:, rng.integers(0, 8)] = 0.0
    return pack(t, heat(rng, t, r, share), nb, snd)
def setup_inputs_spread(rng):
    t, r, nb, snd = parts(rng)
    t = np.minimum(np.maximum(np.exp2(10 + 10 * rng.random((N, 8, 16, 1))).astype(np.int64), 1), 2 ** 20)
    r = np.minimum((np.exp2(20 * rng.random((N, 8, 1, V))) * rng.random((N, 8, 16, V))).astype(np.int64), 2 ** 20 - 1)
    return pack(t, r, nb, snd)
def check_inputs(d):
    bad = []
    for k, lo, hi in (("r0", 0, 2 ** 20 - 1), ("th", 1, 2 ** 20), ("nb", 0, V + (N - 1) * G - 1), ("snd", 0, V - 1)):
        if np.min(d[k]) < lo or np.max(d[k]) > hi: bad.append("range of " + k)
    return bad
def reference(r0, th, nb, snd):
    r = r0.astype(np.int64).reshape(N, 8, 16, V); t = th.astype(np.int64).reshape(N, 8, 16, 1); p = np.zeros((N, 8, 16, V), np.int64)
    nbl = np.stack([gentries(a) for a in nb]).astype(np.int64); sl = np.stack([gentries(a) for a in snd]).astype(np.int64).reshape(N, 8, N - 1, G)
    for rnd in range(RO):
        over = r >= t; s = np.where(over, r >> SH, 0)
        p = p + np.where(over, r - D * s, 0); r = np.where(over, 0, r)
        hot = np.any(over, axis=2)
        come = []
        for a in range(N):
            w = [s[a]]
            for d in range(1, N):
                q = (a - d) % N; ix = sl[q, :, d - 1]
                h = np.take_along_axis(hot[q], ix, 1).astype(np.int64); before = np.add.accumulate(h, axis=1) - h
                v = np.take_along_axis(s[q], ix[:, None, :], 2)
                w.append(np.where(((h == 1) & (before < CAP))[:, None, :], v, 0))
            w = np.concatenate(w, axis=2)
            come.append(np.add.reduce(np.take_along_axis(w, nbl[a][:, None, :], 2).reshape(8, 16, D, V), axis=2))
        r = r + np.stack(come)
    return {"yp": p.reshape(N, 128, V).astype(np.float32), "yr": r.reshape(N, 128, V).astype(np.float32)}

@@ -1,0 +1,377 @@
+from concourse.bass import DstId, RemoteDMATransfer
+from concourse.mybir import AluOpType, ActivationFunctionType
+
+N, V, G, CAP, RO = 4, 2048, 512, 128, 3
+Z = 8
+WN = V + (N - 1) * G
+M = 1.5 * 2 ** 26
+BIG = float(2 ** 23)
+K = 4096.0
+PRM = {
+    "banks": [512, 512, 512, 384, 128],
+    "cuts": [128],
+    "vv": [128, 128, 128],
+    "cs": [768, 512, 512],
+    "rkv": [[], [0, 1], [0, 1]],
+    "f": [256, 0],
+    "sv": [352, 352, 352],
+    "fill": 256,
+    "vcp": [0],
+    "fuse": 1,
+    "link": 2.6, "hop": 0.12, "look": 0.25, "pe": 2.1e-3,
+}
+NB = len(PRM["banks"])
+
+SCRATCH = {}
+for _dt, _bufs in (("int32", (("r0i", V), ("thi", 4), ("nbi", 512), ("sni", 96))),
+                   ("uint16", (("nbo", 512), ("sno", 96))),
+                   ("float32", (("r0f", V), ("bias", 4), ("sn8", 96), ("eye0", 384), ("eye", 384), ("rst", 96), ("cnt", 96), ("sel", 96),
+                                ("pc0", V), ("pc1", V), ("ac0", V), ("ac1", V), ("tmp", V), ("tv", 3 * G))),
+                   ("bfloat16", (("c1", 144), ("ck", 128), ("t1", 144), ("t2", 144), ("t3", 128), ("t4", 128), ("bw", 144), ("lo", 128),
+                                 ("up", 128), ("hot", 96), ("fl", 3 * G)))):
+    for _n, _w in _bufs:
+        SCRATCH[_n] = ("sbuf", [128, _w], _dt)
+for _t in range(RO):
+    for _n, _w, _dt in (("Y", V, "bfloat16"), ("ro", Z + V, "float32"), ("W", WN, "float32"), ("sb", 3 * G, "float32"),
+                        ("of", 96, "uint16"), ("dp", V, "float32")):
+        SCRATCH["%s%d" % (_n, _t)] = ("sbuf", [128, _w], _dt)
+PSUM = ["ps", "q0", "q1"] + ["R%d" % _k for _k in range(NB)]
+for _n in PSUM:
+    SCRATCH[_n] = ("psum", [128, 512], "float32")
+
+NDMA = 24
+SEMAPHORES = ["cv", "cs", "cp", "cg"] + ["arr%d" % t for t in range(RO)] + ["snt%d" % k for k in range(3 * RO)] + \
+             ["d%d" % k for k in range(NDMA)]
+
+
+def engine_plan(topo, src, dsts):
+    off = [d for d in dsts if topo.chip(d) != topo.chip(src)]
+    used = [e for d in off for e in topo.engines(src, d)]
+    plan = {}
+    for d in dsts:
+        free = topo.engines(src, d) if d in off else [e for e in topo.engines(src, d) if e not in used]
+        n = 1
+        while 2 * n <= len(free):
+            n *= 2
+        plan[d] = free[:n]
+    return off, plan
+
+
+def plain(n):
+    return 0.06 + max(64, n) * 1.04e-3
+
+
+def picked(n):
+    return 0.06 + n * 1.62e-3
+
+
+def schedule(ops):
+    hop, look = PRM["hop"], PRM["look"]
+    for o in ops:
+        o["next"] = []
+    for o in ops:
+        for d in o["order"]:
+            d["next"].append(o)
+    for o in reversed(ops):
+        o["tail"] = o["hold"] + o["lag"] + max([hop + x["tail"] for x in o["next"]] + [0.0])
+        o["left"] = len(o["order"])
+        o["ready"] = 0.0
+    free, lane = {}, {}
+    pool = [o for o in ops if o["left"] == 0]
+    while pool:
+        best = None
+        for q in sorted(set(o["q"] for o in pool)):
+            mine = [o for o in pool if o["q"] == q]
+            now = max(free.get(q, 0.0), min(o["ready"] for o in mine))
+            pick = max([o for o in mine if o["ready"] <= now + look], key=lambda o: (o["tail"], -o["n"]))
+            at = max(now, pick["ready"])
+            if best is None or (at, pick["n"]) < (best[0], best[1]["n"]):
+                best = (at, pick)
+        at, o = best
+        pool = [x for x in pool if x is not o]
+        o["at"] = at
+        free[o["q"]] = at + o["hold"]
+        done = at + o["hold"] + o["lag"]
+        if o["lane"]:
+            done = max(done, lane.get(o["lane"][0], 0.0) + o["lane"][1])
+            lane[o["lane"][0]] = done
+        for x in o["next"]:
+            x["ready"] = max(x["ready"], done + (hop if any(d is o for d in x["deps"]) else 0.0))
+            x["left"] -= 1
+            if x["left"] == 0:
+                pool.append(x)
+
+
+def rank_program(g, core, T, topo):
+    rank = T.rank_of(core)
+    if rank is None:
+        return
+    A, F = AluOpType, ActivationFunctionType
+    ops = []
+    queue = {"v": g.vector, "s": g.scalar, "p": g.tensor, "g": g, "y": g.sync}
+    counter = {"v": T.sem.cv, "s": T.sem.cs, "p": T.sem.cp, "g": T.sem.cg}
+    ndma = [0]
+
+    def op(q, hold, fn, reads, writes, kind="c", token=None, lag=0.0, lane=None, after=()):
+        deps = []
+        for o in ops:
+            hit = False
+            for mine, theirs, rr in ((writes, o["w"], 0), (writes, o["r"], 0), (reads, o["w"], 0), (reads, o["r"], 1)):
+                for (n, a, b) in mine:
+                    for (n2, a2, b2) in theirs:
+                        if n == n2 and ((n in PSUM and o["q"] != q) or (not rr and a < b2 and a2 < b)):
+                            hit = True
+            if hit:
+                deps.append(o)
+        if kind == "d":
+            token = (T.sem["d%d" % ndma[0]], 16, "d%d" % ndma[0])
+            ndma[0] += 1
+        o = {"q": q, "hold": hold, "lag": lag, "lane": lane, "fn": fn, "r": reads, "w": writes, "kind": kind, "tok": token,
+             "n": len(ops), "order": deps + list(after), "deps": [d for d in deps if not (d["q"] == "p" and q == "p")]}
+        ops.append(o)
+        return o
+
+    def dma(q, out, src, reads, writes, nbytes, add=False):
+        fn = (lambda: g.dma_start(out(), src(), accum_op=A.add)) if add else (lambda: queue[q].dma_start(out(), src()))
+        move = nbytes / 250e3
+        return op(q, 1.0 if q == "g" else 0.1, fn, reads, writes, "d", lag=2.0 + move, lane=("local", move))
+
+    BANKS = PRM["banks"]
+    start = [sum(BANKS[:k]) for k in range(NB)]
+    banks = [(k, start[k], start[k] + BANKS[k]) for k in range(NB)]
+    dsts = [T.cores[(rank + d) % N] for d in range(1, N)]
+    off, plan = engine_plan(topo, core, dsts)
+    landing = 0
+    for d in range(1, N):
+        src = T.cores[(rank - d) % N]
+        landing += len(engine_plan(topo, src, [T.cores[(rank - d + e) % N] for e in range(1, N)])[1][core])
+    first = 0 if dsts[0] in off else N - 2
+    rest = [j for j in range(N - 1) if j != first]
+    rest_order = sorted(rest, key=lambda j: dsts[j] not in off)
+
+    def R(k, a=None, b=None):
+        if a is None:
+            return T["R%d" % k][:, 0:BANKS[k]]
+        return T["R%d" % k][:, a - start[k]:b - start[k]]
+
+    dma("s", lambda: T.thi[:, 0:1], lambda: T.th[:], [], [("thi", 0, 4)], 512)
+    for k, a, b in banks:
+        dma("y", lambda a=a, b=b: T.r0i[:, a:b], lambda a=a, b=b: T.r0[:, a:b], [], [("r0i", a, b)], 512 * (b - a))
+    dma("s", lambda: T.sni[:], lambda: T.snd[:], [], [("sni", 0, 96)], 512 * 96)
+    dma("y", lambda: T.nbi[:], lambda: T.nb[:], [("r0i", V - 1, V)], [("nbi", 0, 512)], 512 * 512)
+
+    def fill(name, a, b, val, step=1):
+        op("v", plain(b - a), lambda: g.vector.memset(T[name][:, a:b:step] if step > 1 else T[name][:, a:b], val), [], [(name, a, b)])
+
+    fill("eye0", 0, 128, 1.0)
+    fill("eye0", 128, 256, -1.0)
+    fill("eye0", 256, 384, 0.125)
+    fill("c1", 0, 144, 1.0)
+    fill("ck", 0, 128, -K)
+    fill("rst", 0, 96, -1.0e9)
+    for t in range(RO):
+        fill("ro%d" % t, 0, Z, 0.0)
+    fill("rst", 0, 96, CAP * K, 32)
+
+    def sel(out, src, w, pattern, cmp, base, cm):
+        op("g", 0.2 + w * 2.1e-3, lambda: g.affine_select(T[out][:], T[src][:], pattern, cmp, 0.0, base, cm), [(src, 0, w)], [(out, 0, w)])
+
+    sel("eye", "eye0", 384, [[0, 3], [-1, 128]], A.is_equal, 0, 1)
+    sel("t1", "c1", 144, [[0, 9], [1, 16]], A.is_equal, -15, 0)
+    sel("t2", "t1", 144, [[1, 144]], A.is_ge, 0, -1)
+    sel("bw", "t2", 144, [[-1, 144]], A.is_ge, 15, 1)
+    sel("t3", "ck", 128, [[-16, 8], [0, 16]], A.is_ge, 0, 1)
+    sel("lo", "t3", 128, [[1, 128]], A.is_gt, 0, -1)
+    sel("t4", "ck", 128, [[16, 8], [0, 16]], A.is_ge, 15, -1)
+    sel("up", "t4", 128, [[-1, 128]], A.is_ge, 0, 1)
+
+    op("v", plain(1), lambda: g.vector.tensor_scalar(T.bias[:, 0:1], T.thi[:, 0:1], -0.5, -BIG, A.add, A.mult), [("thi", 0, 4)], [("bias", 0, 4)])
+    op("v", plain(96), lambda: g.vector.tensor_copy(T.sno[:], T.sni[:]), [("sni", 0, 96)], [("sno", 0, 96)])
+    op("v", plain(96), lambda: g.vector.tensor_scalar(T.sn8[:], T.sni[:], float(Z), None, A.add), [("sni", 0, 96)], [("sn8", 0, 96)])
+
+    def into(k, eye, src, shift, a, b, begin, end, after=()):
+        op("p", 0.02 + (b - a) * PRM["pe"], lambda: g.tensor.matmul(R(k, a, b), T.eye[:, eye:eye + 128], T[src][:, shift + a:shift + b], begin, end),
+           [("eye", 0, 384), (src, shift + a, shift + b)], [("R%d" % k, 0, 512)], after=after)
+
+    def steps_ab(t, k, a, b):
+        src, rd = (T.r0f[:, a:b], ("r0f", a, b)) if t == 0 else (R(k), ("R%d" % k, 0, 512))
+        op("s", plain(b - a), lambda: g.scalar.activation(T["Y%d" % t][:, a:b], src, F.Relu, bias=T.bias[:, 0:1], scale=BIG),
+           [rd, ("bias", 0, 4)], [("Y%d" % t, a, b)])
+        op("v", plain(b - a), lambda: g.vector.tensor_tensor(T["ro%d" % t][:, Z + a:Z + b], R(k), T["Y%d" % t][:, a:b], A.min),
+           [("R%d" % k, 0, 512), ("Y%d" % t, a, b)], [("ro%d" % t, Z + a, Z + b)])
+
+    for k, a, b in banks:
+        op("v", plain(b - a), lambda a=a, b=b: g.vector.tensor_copy(T.r0f[:, a:b], T.r0i[:, a:b]), [("r0i", a, b)], [("r0f", a, b)])
+        into(k, 0, "r0f", 0, a, b, True, True)
+        steps_ab(0, k, a, b)
+
+    def one_round(t):
+        Y, ro, W, sb, of, dp = ("Y%d" % t, "ro%d" % t, "W%d" % t, "sb%d" % t, "of%d" % t, "dp%d" % t)
+        gate = {}
+
+        def room(blocks, bank, fv):
+            s0, s1 = blocks[0] * G, (blocks[-1] + 1) * G
+            sm, c0, c1, w = s0 + fv, s0 // 16, s1 // 16, (s1 - s0) // 16
+            if fv:
+                op("v", picked(fv), lambda: g.vector.tensor_copy(T.fl[:, s0:sm], T[Y][:, 0:V].indirect(T.sno[:, c0:sm // 16])),
+                   [(Y, 0, V), ("sno", 0, 96)], [("fl", s0, sm)])
+            gate["f"] = op("s", picked(s1 - sm), lambda: g.scalar.activation(T.fl[:, sm:s1], T[Y][:, 0:V].indirect(T.sno[:, sm // 16:c1]), F.Copy),
+                           [(Y, 0, V), ("sno", 0, 96)], [("fl", sm, s1)])
+
+            def seeds():
+                for i in range(16):
+                    ins = g.tensor.matmul(T[bank][:, 0:w], T.bw[:, 15 - i:143 - i], T.fl[:, s0 + i:s1:16], i == 0, i == 15)
+                return ins
+
+            def before():
+                g.tensor.matmul(T[bank][:, 128:128 + w], T.lo[:], T.hot[:, c0:c1], True, False)
+                for j in range(len(blocks)):
+                    ins = g.tensor.matmul(T[bank][:, 129 + 32 * j:160 + 32 * j], T.up[:], T.hot[:, c0 + 32 * j:c0 + 32 * j + 31],
+                                          False, j == len(blocks) - 1)
+                return ins
+
+            op("p", 0.6, seeds, [("bw", 0, 144), ("fl", s0, s1)], [(bank, 0, w)])
+            op("v", plain(w), lambda: g.vector.tensor_scalar(T.hot[:, c0:c1], T[bank][:, 0:w], 1.0, None, A.min), [(bank, 0, w)], [("hot", c0, c1)])
+            gate["p"] = op("p", 0.1, before, [("lo", 0, 128), ("up", 0, 128), ("hot", c0, c1)], [(bank, 128, 128 + w)])
+            op("v", plain(w), lambda: g.vector.tensor_tensor_scan(T.cnt[:, c0:c1], T.rst[:, c0:c1], T[bank][:, 128:128 + w], 0.0, A.max, A.add),
+               [("rst", 0, 96), (bank, 128, 128 + w)], [("cnt", c0, c1)])
+            op("v", plain(2 * w), lambda: g.vector.tensor_tensor(T.sel[:, c0:c1], T.cnt[:, c0:c1], T.sn8[:, c0:c1], A.min),
+               [("cnt", c0, c1), ("sn8", 0, 96)], [("sel", c0, c1)])
+            op("v", plain(w), lambda: g.vector.tensor_scalar(T[of][:, c0:c1], T.sel[:, c0:c1], 0.0, None, A.max), [("sel", c0, c1)], [(of, c0, c1)])
+
+        def block(j, n):
+            a, m, b = j * G, j * G + PRM["sv"][n], (j + 1) * G
+            rd = [(ro, 0, Z + V), (of, a // 16, b // 16)]
+            gate["v"] = op("v", picked(m - a),
+                           lambda: g.vector.tensor_scalar(T[sb][:, a:m], T[ro][:, 0:Z + V].indirect(T[of][:, a // 16:m // 16]), -3.5, M, A.add, A.add),
+                           rd, [(sb, a, m)])
+            op("s", picked(b - m), lambda: g.scalar.activation(T.tv[:, m:b], T[ro][:, 0:Z + V].indirect(T[of][:, m // 16:b // 16]), F.Identity, bias=-3.5),
+               rd, [("tv", m, b)])
+            gate["s"] = op("s", plain(b - m), lambda: g.scalar.activation(T[sb][:, m:b], T.tv[:, m:b], F.Identity, bias=M), [("tv", m, b)], [(sb, m, b)])
+
+        def send(js, n):
+            name = "snt%d" % (3 * t + n)
+
+            def fn():
+                trs = []
+                for j in js:
+                    rid, pid, _ = topo.addr(dsts[j])
+                    trs.append(RemoteDMATransfer(dst_ids=[DstId(rid=rid, pnc=pid)], dma_engine_mask=sum(1 << e for e in plan[dsts[j]]),
+                                                 remote_sem=T.sem["arr%d" % t], src=T[sb][:, j * G:(j + 1) * G], dst=T[W][:, V + j * G:V + (j + 1) * G]))
+                return g.remote_dma_fused(trs, local_sem=T.sem[name])
+            return op("g", 0.8, fn, [(sb, j * G, (j + 1) * G) for j in js], [], "r", (T.sem[name], sum(len(plan[dsts[j]]) for j in js), name),
+                      1.5 + PRM["link"], (plan[dsts[js[0]]][0], PRM["link"]))
+
+        room([first], "ps", PRM["f"][0])
+        block(first, 0)
+        sends = [send([first], 0)]
+        room(rest, "q0", PRM["f"][1])
+        block(rest_order[0], 1)
+        block(rest_order[1], 2)
+        sends += [send(rest_order, 1)] if PRM["fuse"] else [send(rest_order[:1], 1), send(rest_order[1:], 2)]
+        for x, y in zip(sends[:-1], sends[1:]):
+            y["order"].append(x)
+        op("x", 0.0, None, [], [(W, V, WN)], "x", (T.sem["arr%d" % t], landing, "arr%d" % t), after=sends)
+
+        if t == 0:
+            op("v", plain(512), lambda: g.vector.tensor_copy(T.nbo[:], T.nbi[:]), [("nbi", 0, 512)], [("nbo", 0, 512)], after=[gate["v"]])
+        CS, FL = PRM["cs"][t], PRM["fill"]
+        for a in range(V - CS, V, FL):
+            b = min(V, a + FL)
+            op("s", plain(b - a), lambda a=a, b=b: g.scalar.activation(T.tmp[:, a:b], T[ro][:, Z + a:Z + b], F.Identity, bias=-3.5),
+               [(ro, Z + a, Z + b)], [("tmp", a, b)])
+            op("s", plain(b - a), lambda a=a, b=b: g.scalar.activation(T[W][:, a:b], T.tmp[:, a:b], F.Identity, bias=M), [("tmp", a, b)], [(W, a, b)])
+        for a in range(0, V - CS, FL):
+            b = min(V - CS, a + FL)
+            op("v", plain(b - a), lambda a=a, b=b: g.vector.tensor_scalar(T[W][:, a:b], T[ro][:, Z + a:Z + b], -3.5, M, A.add, A.add),
+               [(ro, Z + a, Z + b)], [(W, a, b)], after=[gate["v"]])
+        for k, a, b in banks:
+            if k in PRM["rkv"][t]:
+                op("v", plain(b - a), lambda k=k, a=a, b=b: g.vector.tensor_tensor(T.r0f[:, a:b], R(k), T[ro][:, Z + a:Z + b], A.subtract),
+                   [("R%d" % k, 0, 512), (ro, Z + a, Z + b)], [("r0f", a, b)], after=[gate["v"]])
+                into(k, 0, "r0f", 0, a, b, True, False, [gate["p"]])
+                continue
+            if t:
+                op("s", plain(b - a), lambda k=k, a=a, b=b: g.scalar.activation(T.r0f[:, a:b], R(k), F.Copy), [("R%d" % k, 0, 512)], [("r0f", a, b)],
+                   after=[gate["f"]])
+            into(k, 0, "r0f", 0, a, b, True, False, [gate["p"]])
+            into(k, 128, ro, Z, a, b, False, False)
+        for j in range(4):
+            a, b, qn = 512 * j, 512 * j + 512, ("q1", "ps", "q0")[j % 3]
+            op("s", plain(512), lambda a=a, b=b, qn=qn: g.scalar.activation(T[qn][:], T[W][:, a:b], F.Identity, bias=M / 2, scale=-0.5),
+               [(W, a, b)], [(qn, 0, 512)], after=[gate["s"]])
+            op("v", plain(512), lambda a=a, b=b, qn=qn: g.vector.tensor_tensor(T[dp][:, a:b], T[qn][:], T[ro][:, Z + a:Z + b], A.add),
+               [(qn, 0, 512), (ro, Z + a, Z + b)], [(dp, a, b)])
+        dma("g" if t else "y", lambda: T.yp[:], lambda: T[dp][:], [(dp, 0, V), (W, V, WN)], [("yp", 0, V)], (1024 if t else 512) * V, t > 0)
+
+        VV = PRM["vv"][t]
+        cuts = sorted(set([0, VV, V] + start + PRM["cuts"]))
+        prev = {}
+
+        def gather(q, out, a, b, i, shift, plus=None):
+            win = lambda: T[W][:, 0:WN].indirect(T.nbo[:, i * 128 + a // 16:i * 128 + b // 16])
+            rd = [(W, 0, WN), ("nbo", 0, 512)]
+            if q == "s":
+                fn = lambda: g.scalar.activation(T[out][:, a:b], win(), F.Identity, bias=shift)
+            elif plus is None:
+                fn = lambda: g.vector.tensor_scalar(T[out][:, a:b], win(), shift, None, A.add)
+            else:
+                fn = lambda: g.vector.tensor_tensor(T[out][:, a:b], win(), T[plus][:, a:b], A.add)
+                rd = rd + [(plus, a, b)]
+            prev[q] = op(q, picked(b - a), fn, rd, [(out, a, b)], after=[prev[q]] if q in prev else [])
+
+        def store(k):
+            _, x, y = banks[k]
+            q = "v" if k in PRM["vcp"] else "s"
+            fn = (lambda: g.vector.tensor_copy(T.r0f[:, x:y], R(k))) if q == "v" else (lambda: g.scalar.activation(T.r0f[:, x:y], R(k), F.Copy))
+            prev[q] = op(q, plain(y - x), fn, [("R%d" % k, 0, 512)], [("r0f", x, y)], after=[prev[q]])
+            dma("y", lambda: T.yr[:, x:y], lambda: T.r0f[:, x:y], [("r0f", x, y)], [("yr", x, y)], 512 * (y - x))
+
+        for a, b in zip(cuts[:-1], cuts[1:]):
+            k = max(x for x in range(NB) if start[x] <= a)
+            closing = b == start[k] + BANKS[k]
+            for i in range(2):
+                gather("v" if a < VV else "s", "pc%d" % i, a, b, 2 + i, -2 * M)
+            for i in range(2):
+                gather("v", "ac%d" % i, a, b, i, None, "pc%d" % i)
+                into(k, 256, "ac%d" % i, 0, a, b, False, closing and i == 1)
+            if closing and t < RO - 1:
+                steps_ab(t + 1, k, banks[k][1], banks[k][2])
+            elif closing:
+                for kk in ([k - 1] if k else []) + ([k] if k == NB - 1 else []):
+                    store(kk)
+
+    for t in range(RO):
+        one_round(t)
+
+    schedule(ops)
+    lists, total = {}, {}
+    for q in queue:
+        lists[q] = sorted([o for o in ops if o["q"] == q], key=lambda o: (o["at"], o["n"]))
+        n = 0
+        for o in lists[q]:
+            if o["kind"] == "c":
+                n += 1
+                o["tok"] = (counter[q], n, q)
+        total[q] = n
+    for q in queue:
+        seen = {}
+        for o in lists[q]:
+            need = {}
+            for d in o["deps"]:
+                sem, val, name = d["tok"]
+                if val > seen.get(name, 0) and val > need.get(name, (None, 0))[1]:
+                    need[name] = (sem, val)
+            for name in need:
+                queue[q].wait_ge(need[name][0], need[name][1])
+                seen[name] = need[name][1]
+            ins = o["fn"]()
+            if o["kind"] == "c":
+                ins.then_inc(counter[q], 1)
+            elif o["kind"] == "d":
+                ins.then_inc(o["tok"][0], 16)
+    for q in counter:
+        g.wait_ge(counter[q], total[q])
+    for o in ops:
+        if o["kind"] in ("d", "r", "x"):
+            g.wait_ge(o["tok"][0], o["tok"][1])

@@ -4,65 +4,87 @@ from concourse.mybir import AluOpType, ActivationFunctionType
 N, V, G, CAP, RO = 4, 2048, 512, 128, 3
 Z = 8
 WN = V + (N - 1) * G
-M = 1.5 * 2 ** 26
 BIG = float(2 ** 23)
 K = 4096.0
+EIGHTH, DOWN = 0.125, -0.4375
 PRM = {
     "banks": [512, 512, 512, 384, 128],
     "cuts": [128],
-    "vv": [128, 128, 128],
-    "cs": [768, 512, 512],
-    "rkv": [[], [0, 1], [0, 1]],
-    "f": [256, 0],
-    "sv": [352, 352, 352],
+    "early": 128,
+    "f": [256, 256],
+    "ev": 0,
+    "sv": [192, 192, 192],
+    "wv": [0, 0, 0],
+    "cv": [0, 1, 2, 3, 4],
+    "rv": [[], [0, 1, 2, 3, 4], [0, 1, 2, 3, 4]],
+    "add": [[], [], [1, 3, 4]],
+    "pd": [0, 0, 0],
     "fill": 256,
-    "vcp": [0],
-    "fuse": 1,
-    "link": 2.6, "hop": 0.12, "look": 0.25, "pe": 2.1e-3,
+    "fac": 1.25, "gat": 1.56, "link": 1.6, "lat": 1.5, "issue": 0.6, "hop": 0.1, "look": 0.25, "dma": 300e3,
 }
 NB = len(PRM["banks"])
 
 SCRATCH = {}
 for _dt, _bufs in (("int32", (("r0i", V), ("thi", 4), ("nbi", 512), ("sni", 96))),
-                   ("uint16", (("nbo", 512), ("sno", 96))),
-                   ("float32", (("r0f", V), ("bias", 4), ("sn8", 96), ("eye0", 384), ("eye", 384), ("rst", 96), ("cnt", 96), ("sel", 96),
-                                ("pc0", V), ("pc1", V), ("ac0", V), ("ac1", V), ("tmp", V), ("tv", 3 * G))),
+                   ("uint16", (("nbo", 512), ("sno", 96), ("sne", 24))),
+                   ("float32", (("r0f", V), ("bias", 4), ("sn8", 96), ("eye0", 256), ("eye", 256), ("rst", 96), ("cnt", 96), ("sel", 96),
+                                ("pc0", V), ("pc1", V), ("ac0", V), ("ac1", V))),
                    ("bfloat16", (("c1", 144), ("ck", 128), ("t1", 144), ("t2", 144), ("t3", 128), ("t4", 128), ("bw", 144), ("lo", 128),
-                                 ("up", 128), ("hot", 96), ("fl", 3 * G)))):
+                                 ("up", 128), ("hot", 96), ("fl", 3 * G), ("Y", V)))):
     for _n, _w in _bufs:
         SCRATCH[_n] = ("sbuf", [128, _w], _dt)
 for _t in range(RO):
-    for _n, _w, _dt in (("Y", V, "bfloat16"), ("ro", Z + V, "float32"), ("W", WN, "float32"), ("sb", 3 * G, "float32"),
-                        ("of", 96, "uint16"), ("dp", V, "float32")):
+    for _n, _w, _dt in (("ro", Z + V, "float32"), ("W", WN, "int32"), ("sb", 3 * G, "int32"), ("of", 96, "uint16"), ("dp", V, "float32")):
         SCRATCH["%s%d" % (_n, _t)] = ("sbuf", [128, _w], _dt)
-PSUM = ["ps", "q0", "q1"] + ["R%d" % _k for _k in range(NB)]
+PSUM = ["q0", "q1", "q2"] + ["R%d" % _k for _k in range(NB)]
 for _n in PSUM:
     SCRATCH[_n] = ("psum", [128, 512], "float32")
 
-NDMA = 24
+NDMA = 32
 SEMAPHORES = ["cv", "cs", "cp", "cg"] + ["arr%d" % t for t in range(RO)] + ["snt%d" % k for k in range(3 * RO)] + \
              ["d%d" % k for k in range(NDMA)]
 
 
+def split(engines, parts):
+    n = 1
+    while 2 * n * parts <= len(engines):
+        n *= 2
+    return [engines[k * n:(k + 1) * n] for k in range(parts)]
+
+
 def engine_plan(topo, src, dsts):
     off = [d for d in dsts if topo.chip(d) != topo.chip(src)]
-    used = [e for d in off for e in topo.engines(src, d)]
     plan = {}
+    if off:
+        plan.update(zip(off, split(topo.engines(src, off[0]), len(off))))
+    far = [c for c in range(48) if topo.chip(c) != topo.chip(src) and topo.may_write(src, c)][0]
     for d in dsts:
-        free = topo.engines(src, d) if d in off else [e for e in topo.engines(src, d) if e not in used]
-        n = 1
-        while 2 * n <= len(free):
-            n *= 2
-        plan[d] = free[:n]
-    return off, plan
+        if d not in off:
+            plan[d] = split([e for e in topo.engines(src, d) if e not in topo.engines(src, far)], 1)[0]
+    return plan
 
 
-def plain(n):
-    return 0.06 + max(64, n) * 1.04e-3
+def calls_of(topo, cores, rank):
+    off = [j for j in range(N - 1) if topo.chip(cores[(rank + 1 + j) % N]) != topo.chip(cores[rank])]
+    first = 0 if 0 in off else N - 2
+    rest = sorted([j for j in range(N - 1) if j != first], key=lambda j: j not in off)
+    E = PRM["early"]
+    return ([([first] + rest, 0, E)] if E else []) + [([first], E, G), (rest, E, G)]
 
 
-def picked(n):
-    return 0.06 + n * 1.62e-3
+def hold_of(q, cost):
+    kind, n, f = cost[0], cost[1], PRM["fac"]
+    if kind == "plain":
+        return 0.055 + max(64, n) * 0.83e-3 * f
+    if kind == "pick":
+        return 0.06 + n * 0.83e-3 * f * PRM["gat"]
+    if kind == "pe":
+        return 0.015 + n * 0.417e-3 * f
+    if kind == "g":
+        return 0.17 + n * 1.66e-3 * f
+    if kind == "dma":
+        return 1.0 if q == "g" else 0.1
+    return PRM["issue"] if kind == "rem" else 0.0
 
 
 def schedule(ops):
@@ -112,7 +134,7 @@ def rank_program(g, core, T, topo):
     counter = {"v": T.sem.cv, "s": T.sem.cs, "p": T.sem.cp, "g": T.sem.cg}
     ndma = [0]
 
-    def op(q, hold, fn, reads, writes, kind="c", token=None, lag=0.0, lane=None, after=()):
+    def op(q, cost, fn, reads, writes, kind="c", token=None, lag=0.0, lane=None, after=()):
         deps = []
         for o in ops:
             hit = False
@@ -126,28 +148,35 @@ def rank_program(g, core, T, topo):
         if kind == "d":
             token = (T.sem["d%d" % ndma[0]], 16, "d%d" % ndma[0])
             ndma[0] += 1
-        o = {"q": q, "hold": hold, "lag": lag, "lane": lane, "fn": fn, "r": reads, "w": writes, "kind": kind, "tok": token,
-             "n": len(ops), "order": deps + list(after), "deps": [d for d in deps if not (d["q"] == "p" and q == "p")]}
+        o = {"q": q, "cost": cost, "hold": hold_of(q, cost), "lag": lag, "lane": lane, "fn": fn, "r": reads, "w": writes, "kind": kind,
+             "tok": token, "n": len(ops), "order": deps + list(after), "deps": [d for d in deps if not (d["q"] == "p" and q == "p")]}
         ops.append(o)
         return o
 
     def dma(q, out, src, reads, writes, nbytes, add=False):
         fn = (lambda: g.dma_start(out(), src(), accum_op=A.add)) if add else (lambda: queue[q].dma_start(out(), src()))
-        move = nbytes / 250e3
-        return op(q, 1.0 if q == "g" else 0.1, fn, reads, writes, "d", lag=2.0 + move, lane=("local", move))
+        move = nbytes / PRM["dma"]
+        return op(q, ("dma", nbytes), fn, reads, writes, "d", lag=1.7 + move, lane=("local", move))
+
+    def affine(q, out, src, scale, shift, cost, reads, writes, after=()):
+        if q == "v":
+            fn = lambda: g.vector.tensor_scalar(out(), src(), scale, shift, A.mult, A.add)
+        else:
+            fn = lambda: g.scalar.activation(out(), src(), F.Identity, bias=shift, scale=scale)
+        return op(q, cost, fn, reads, writes, after=after)
 
     BANKS = PRM["banks"]
     start = [sum(BANKS[:k]) for k in range(NB)]
     banks = [(k, start[k], start[k] + BANKS[k]) for k in range(NB)]
     dsts = [T.cores[(rank + d) % N] for d in range(1, N)]
-    off, plan = engine_plan(topo, core, dsts)
+    calls = calls_of(topo, T.cores, rank)
     landing = 0
     for d in range(1, N):
-        src = T.cores[(rank - d) % N]
-        landing += len(engine_plan(topo, src, [T.cores[(rank - d + e) % N] for e in range(1, N)])[1][core])
-    first = 0 if dsts[0] in off else N - 2
-    rest = [j for j in range(N - 1) if j != first]
-    rest_order = sorted(rest, key=lambda j: dsts[j] not in off)
+        q = (rank - d) % N
+        for js, _, _ in calls_of(topo, T.cores, q):
+            landing += len(engine_plan(topo, T.cores[q], [T.cores[(q + 1 + j) % N] for j in js]).get(core, []))
+    E = PRM["early"]
+    (first,), rest = calls[-2][0], calls[-1][0]
 
     def R(k, a=None, b=None):
         if a is None:
@@ -161,12 +190,11 @@ def rank_program(g, core, T, topo):
     dma("y", lambda: T.nbi[:], lambda: T.nb[:], [("r0i", V - 1, V)], [("nbi", 0, 512)], 512 * 512)
 
     def fill(name, a, b, val, step=1):
-        op("v", plain(b - a), lambda: g.vector.memset(T[name][:, a:b:step] if step > 1 else T[name][:, a:b], val), [], [(name, a, b)])
+        op("v", ("plain", b - a), lambda: g.vector.memset(T[name][:, a:b:step] if step > 1 else T[name][:, a:b], val), [], [(name, a, b)])
 
+    fill("c1", 0, 144, 1.0)
     fill("eye0", 0, 128, 1.0)
     fill("eye0", 128, 256, -1.0)
-    fill("eye0", 256, 384, 0.125)
-    fill("c1", 0, 144, 1.0)
     fill("ck", 0, 128, -K)
     fill("rst", 0, 96, -1.0e9)
     for t in range(RO):
@@ -174,9 +202,9 @@ def rank_program(g, core, T, topo):
     fill("rst", 0, 96, CAP * K, 32)
 
     def sel(out, src, w, pattern, cmp, base, cm):
-        op("g", 0.2 + w * 2.1e-3, lambda: g.affine_select(T[out][:], T[src][:], pattern, cmp, 0.0, base, cm), [(src, 0, w)], [(out, 0, w)])
+        op("g", ("g", w), lambda: g.affine_select(T[out][:], T[src][:], pattern, cmp, 0.0, base, cm), [(src, 0, w)], [(out, 0, w)])
 
-    sel("eye", "eye0", 384, [[0, 3], [-1, 128]], A.is_equal, 0, 1)
+    sel("eye", "eye0", 256, [[0, 2], [-1, 128]], A.is_equal, 0, 1)
     sel("t1", "c1", 144, [[0, 9], [1, 16]], A.is_equal, -15, 0)
     sel("t2", "t1", 144, [[1, 144]], A.is_ge, 0, -1)
     sel("bw", "t2", 144, [[-1, 144]], A.is_ge, 15, 1)
@@ -185,38 +213,49 @@ def rank_program(g, core, T, topo):
     sel("t4", "ck", 128, [[16, 8], [0, 16]], A.is_ge, 15, -1)
     sel("up", "t4", 128, [[-1, 128]], A.is_ge, 0, 1)
 
-    op("v", plain(1), lambda: g.vector.tensor_scalar(T.bias[:, 0:1], T.thi[:, 0:1], -0.5, -BIG, A.add, A.mult), [("thi", 0, 4)], [("bias", 0, 4)])
-    op("v", plain(96), lambda: g.vector.tensor_copy(T.sno[:], T.sni[:]), [("sni", 0, 96)], [("sno", 0, 96)])
-    op("v", plain(96), lambda: g.vector.tensor_scalar(T.sn8[:], T.sni[:], float(Z), None, A.add), [("sni", 0, 96)], [("sn8", 0, 96)])
+    op("v", ("plain", 1), lambda: g.vector.tensor_scalar(T.bias[:, 0:1], T.thi[:, 0:1], -0.5, -BIG, A.add, A.mult), [("thi", 0, 4)], [("bias", 0, 4)])
+    op("v", ("plain", 96), lambda: g.vector.tensor_copy(T.sno[:], T.sni[:]), [("sni", 0, 96)], [("sno", 0, 96)])
+    op("v", ("plain", 96), lambda: g.vector.tensor_scalar(T.sn8[:], T.sni[:], float(Z), None, A.add), [("sni", 0, 96)], [("sn8", 0, 96)])
+    for j in range(N - 1 if E else 0):
+        c, w = j * E // 16, E // 16
+        op("v", ("plain", w), lambda j=j, c=c, w=w: g.vector.tensor_scalar(T.sne[:, c:c + w], T.sni[:, 32 * j:32 * j + w], float(Z), None, A.add),
+           [("sni", 0, 96)], [("sne", c, c + w)])
 
     def into(k, eye, src, shift, a, b, begin, end, after=()):
-        op("p", 0.02 + (b - a) * PRM["pe"], lambda: g.tensor.matmul(R(k, a, b), T.eye[:, eye:eye + 128], T[src][:, shift + a:shift + b], begin, end),
-           [("eye", 0, 384), (src, shift + a, shift + b)], [("R%d" % k, 0, 512)], after=after)
+        op("p", ("pe", 4 * (b - a)), lambda: g.tensor.matmul(R(k, a, b), T.eye[:, eye:eye + 128], T[src][:, shift + a:shift + b], begin, end),
+           [("eye", 0, 256), (src, shift + a, shift + b)], [("R%d" % k, 0, 512)], after=after)
 
     def steps_ab(t, k, a, b):
-        src, rd = (T.r0f[:, a:b], ("r0f", a, b)) if t == 0 else (R(k), ("R%d" % k, 0, 512))
-        op("s", plain(b - a), lambda: g.scalar.activation(T["Y%d" % t][:, a:b], src, F.Relu, bias=T.bias[:, 0:1], scale=BIG),
-           [rd, ("bias", 0, 4)], [("Y%d" % t, a, b)])
-        op("v", plain(b - a), lambda: g.vector.tensor_tensor(T["ro%d" % t][:, Z + a:Z + b], R(k), T["Y%d" % t][:, a:b], A.min),
-           [("R%d" % k, 0, 512), ("Y%d" % t, a, b)], [("ro%d" % t, Z + a, Z + b)])
+        if t == 0:
+            qn = "q%d" % (k % 3)
+            r, rr, y, yy = T.r0i[:, a:b], ("r0i", a, b), T[qn][:, 0:b - a], (qn, 0, 512)
+        else:
+            r, rr, y, yy = R(k), ("R%d" % k, 0, 512), T.Y[:, a:b], ("Y", a, b)
+        op("s", ("plain", b - a), lambda: g.scalar.activation(y, r, F.Relu, bias=T.bias[:, 0:1], scale=BIG), [rr, ("bias", 0, 4)], [yy])
+        op("v", ("plain", b - a), lambda: g.vector.tensor_tensor(T["ro%d" % t][:, Z + a:Z + b], r, y, A.min), [rr, yy], [("ro%d" % t, Z + a, Z + b)])
 
     for k, a, b in banks:
-        op("v", plain(b - a), lambda a=a, b=b: g.vector.tensor_copy(T.r0f[:, a:b], T.r0i[:, a:b]), [("r0i", a, b)], [("r0f", a, b)])
-        into(k, 0, "r0f", 0, a, b, True, True)
         steps_ab(0, k, a, b)
+    for k, a, b in banks:
+        affine("v" if k in PRM["cv"] else "s", lambda a=a, b=b: T.r0f[:, a:b], lambda a=a, b=b: T.r0i[:, a:b], 1.0, 0.0, ("plain", b - a),
+               [("r0i", a, b)], [("r0f", a, b)])
+        into(k, 0, "r0f", 0, a, b, True, False)
 
     def one_round(t):
-        Y, ro, W, sb, of, dp = ("Y%d" % t, "ro%d" % t, "W%d" % t, "sb%d" % t, "of%d" % t, "dp%d" % t)
+        ro, W, sb, of, dp = ("ro%d" % t, "W%d" % t, "sb%d" % t, "of%d" % t, "dp%d" % t)
         gate = {}
+        over, shift = (ro, Z) if t == 0 else ("Y", 0)
+
+        def place(j, a):
+            return j * E + a if a < E else (N - 1) * E + j * (G - E) + a - E
 
         def room(blocks, bank, fv):
-            s0, s1 = blocks[0] * G, (blocks[-1] + 1) * G
+            s0, s1 = min(blocks) * G, (max(blocks) + 1) * G
             sm, c0, c1, w = s0 + fv, s0 // 16, s1 // 16, (s1 - s0) // 16
-            if fv:
-                op("v", picked(fv), lambda: g.vector.tensor_copy(T.fl[:, s0:sm], T[Y][:, 0:V].indirect(T.sno[:, c0:sm // 16])),
-                   [(Y, 0, V), ("sno", 0, 96)], [("fl", s0, sm)])
-            gate["f"] = op("s", picked(s1 - sm), lambda: g.scalar.activation(T.fl[:, sm:s1], T[Y][:, 0:V].indirect(T.sno[:, sm // 16:c1]), F.Copy),
-                           [(Y, 0, V), ("sno", 0, 96)], [("fl", sm, s1)])
+            for q, a, b in (("v", s0, sm), ("s", sm, s1)):
+                if a < b:
+                    gate["f" + q] = affine(q, lambda a=a, b=b: T.fl[:, a:b], lambda a=a, b=b: T[over][:, shift:shift + V].indirect(T.sno[:, a // 16:b // 16]),
+                                           1.0, 0.0, ("pick", b - a), [(over, shift, shift + V), ("sno", 0, 96)], [("fl", a, b)])
 
             def seeds():
                 for i in range(16):
@@ -230,116 +269,123 @@ def rank_program(g, core, T, topo):
                                           False, j == len(blocks) - 1)
                 return ins
 
-            op("p", 0.6, seeds, [("bw", 0, 144), ("fl", s0, s1)], [(bank, 0, w)])
-            op("v", plain(w), lambda: g.vector.tensor_scalar(T.hot[:, c0:c1], T[bank][:, 0:w], 1.0, None, A.min), [(bank, 0, w)], [("hot", c0, c1)])
-            gate["p"] = op("p", 0.1, before, [("lo", 0, 128), ("up", 0, 128), ("hot", c0, c1)], [(bank, 128, 128 + w)])
-            op("v", plain(w), lambda: g.vector.tensor_tensor_scan(T.cnt[:, c0:c1], T.rst[:, c0:c1], T[bank][:, 128:128 + w], 0.0, A.max, A.add),
+            op("p", ("pe", 1100), seeds, [("bw", 0, 144), ("fl", s0, s1)], [(bank, 0, w)])
+            op("v", ("plain", w), lambda: g.vector.tensor_scalar(T.hot[:, c0:c1], T[bank][:, 0:w], 1.0, None, A.min), [(bank, 0, w)], [("hot", c0, c1)])
+            gate["p"] = op("p", ("pe", 192), before, [("lo", 0, 128), ("up", 0, 128), ("hot", c0, c1)], [(bank, 128, 128 + w)])
+            op("v", ("plain", w), lambda: g.vector.tensor_tensor_scan(T.cnt[:, c0:c1], T.rst[:, c0:c1], T[bank][:, 128:128 + w], 0.0, A.max, A.add),
                [("rst", 0, 96), (bank, 128, 128 + w)], [("cnt", c0, c1)])
-            op("v", plain(2 * w), lambda: g.vector.tensor_tensor(T.sel[:, c0:c1], T.cnt[:, c0:c1], T.sn8[:, c0:c1], A.min),
+            op("v", ("plain", 2 * w), lambda: g.vector.tensor_tensor(T.sel[:, c0:c1], T.cnt[:, c0:c1], T.sn8[:, c0:c1], A.min),
                [("cnt", c0, c1), ("sn8", 0, 96)], [("sel", c0, c1)])
-            op("v", plain(w), lambda: g.vector.tensor_scalar(T[of][:, c0:c1], T.sel[:, c0:c1], 0.0, None, A.max), [("sel", c0, c1)], [(of, c0, c1)])
+            op("v", ("plain", w), lambda: g.vector.tensor_scalar(T[of][:, c0:c1], T.sel[:, c0:c1], 0.0, None, A.max), [("sel", c0, c1)], [(of, c0, c1)])
 
-        def block(j, n):
-            a, m, b = j * G, j * G + PRM["sv"][n], (j + 1) * G
-            rd = [(ro, 0, Z + V), (of, a // 16, b // 16)]
-            gate["v"] = op("v", picked(m - a),
-                           lambda: g.vector.tensor_scalar(T[sb][:, a:m], T[ro][:, 0:Z + V].indirect(T[of][:, a // 16:m // 16]), -3.5, M, A.add, A.add),
-                           rd, [(sb, a, m)])
-            op("s", picked(b - m), lambda: g.scalar.activation(T.tv[:, m:b], T[ro][:, 0:Z + V].indirect(T[of][:, m // 16:b // 16]), F.Identity, bias=-3.5),
-               rd, [("tv", m, b)])
-            gate["s"] = op("s", plain(b - m), lambda: g.scalar.activation(T[sb][:, m:b], T.tv[:, m:b], F.Identity, bias=M), [("tv", m, b)], [(sb, m, b)])
+        def values(tile, col, a, b, nv, after=()):
+            for q, x, y in (("v", a, a + nv), ("s", a + nv, b)):
+                if x < y:
+                    c0, c1 = col + (x - a) // 16, col + (y - a) // 16
+                    gate[q] = affine(q, lambda x=x, y=y: T[sb][:, x:y], lambda c0=c0, c1=c1: T[ro][:, 0:Z + V].indirect(T[tile][:, c0:c1]),
+                                     EIGHTH, DOWN, ("pick", y - x), [(ro, 0, Z + V), (tile, c0, c1)], [(sb, x, y)], after)
 
-        def send(js, n):
+        def send(n):
+            js, a, b = calls[n]
             name = "snt%d" % (3 * t + n)
+            plan = engine_plan(topo, core, [dsts[j] for j in js])
+            units = sum(topo.chip(dsts[j]) != topo.chip(core) for j in js) * (b - a) / G
 
             def fn():
                 trs = []
                 for j in js:
                     rid, pid, _ = topo.addr(dsts[j])
                     trs.append(RemoteDMATransfer(dst_ids=[DstId(rid=rid, pnc=pid)], dma_engine_mask=sum(1 << e for e in plan[dsts[j]]),
-                                                 remote_sem=T.sem["arr%d" % t], src=T[sb][:, j * G:(j + 1) * G], dst=T[W][:, V + j * G:V + (j + 1) * G]))
+                                                 remote_sem=T.sem["arr%d" % t], src=T[sb][:, place(j, a):place(j, a) + b - a],
+                                                 dst=T[W][:, V + j * G + a:V + j * G + b]))
                 return g.remote_dma_fused(trs, local_sem=T.sem[name])
-            return op("g", 0.8, fn, [(sb, j * G, (j + 1) * G) for j in js], [], "r", (T.sem[name], sum(len(plan[dsts[j]]) for j in js), name),
-                      1.5 + PRM["link"], (plan[dsts[js[0]]][0], PRM["link"]))
+            return op("g", ("rem", units), fn, [(sb, place(j, a), place(j, a) + b - a) for j in js], [], "r",
+                      (T.sem[name], sum(len(plan[dsts[j]]) for j in js), name), PRM["lat"] + units * PRM["link"], ("link", units * PRM["link"]))
 
-        room([first], "ps", PRM["f"][0])
-        block(first, 0)
-        sends = [send([first], 0)]
-        room(rest, "q0", PRM["f"][1])
-        block(rest_order[0], 1)
-        block(rest_order[1], 2)
-        sends += [send(rest_order, 1)] if PRM["fuse"] else [send(rest_order[:1], 1), send(rest_order[1:], 2)]
+        sends = []
+        room([first], "q0", PRM["f"][0])
+        if E:
+            values("sne", 0, 0, (N - 1) * E, PRM["ev"], [gate[x] for x in ("fv", "fs") if x in gate])
+            sends.append(send(0))
+        values(of, (first * G + E) // 16, place(first, E), place(first, E) + G - E, PRM["sv"][0])
+        sends.append(send(len(sends)))
+        room(rest, "q1", PRM["f"][1])
+        for n, j in enumerate(rest):
+            values(of, (j * G + E) // 16, place(j, E), place(j, E) + G - E, PRM["sv"][1 + n])
+        sends.append(send(len(sends)))
         for x, y in zip(sends[:-1], sends[1:]):
             y["order"].append(x)
-        op("x", 0.0, None, [], [(W, V, WN)], "x", (T.sem["arr%d" % t], landing, "arr%d" % t), after=sends)
+        op("x", ("x", 0), None, [], [(W, V, WN)], "x", (T.sem["arr%d" % t], landing, "arr%d" % t), after=sends)
 
         if t == 0:
-            op("v", plain(512), lambda: g.vector.tensor_copy(T.nbo[:], T.nbi[:]), [("nbi", 0, 512)], [("nbo", 0, 512)], after=[gate["v"]])
-        CS, FL = PRM["cs"][t], PRM["fill"]
-        for a in range(V - CS, V, FL):
-            b = min(V, a + FL)
-            op("s", plain(b - a), lambda a=a, b=b: g.scalar.activation(T.tmp[:, a:b], T[ro][:, Z + a:Z + b], F.Identity, bias=-3.5),
-               [(ro, Z + a, Z + b)], [("tmp", a, b)])
-            op("s", plain(b - a), lambda a=a, b=b: g.scalar.activation(T[W][:, a:b], T.tmp[:, a:b], F.Identity, bias=M), [("tmp", a, b)], [(W, a, b)])
-        for a in range(0, V - CS, FL):
-            b = min(V - CS, a + FL)
-            op("v", plain(b - a), lambda a=a, b=b: g.vector.tensor_scalar(T[W][:, a:b], T[ro][:, Z + a:Z + b], -3.5, M, A.add, A.add),
-               [(ro, Z + a, Z + b)], [(W, a, b)], after=[gate["v"]])
+            op("v", ("plain", 512), lambda: g.vector.tensor_copy(T.nbo[:], T.nbi[:]), [("nbi", 0, 512)], [("nbo", 0, 512)])
+        FL = PRM["fill"]
+        for a in range(0, V, FL):
+            affine("v" if a < PRM["wv"][t] else "s", lambda a=a: T[W][:, a:a + FL], lambda a=a: T[ro][:, Z + a:Z + a + FL], EIGHTH, DOWN, ("plain", FL),
+                   [(ro, Z + a, Z + a + FL)], [(W, a, a + FL)], [gate["fs"]])
         for k, a, b in banks:
-            if k in PRM["rkv"][t]:
-                op("v", plain(b - a), lambda k=k, a=a, b=b: g.vector.tensor_tensor(T.r0f[:, a:b], R(k), T[ro][:, Z + a:Z + b], A.subtract),
-                   [("R%d" % k, 0, 512), (ro, Z + a, Z + b)], [("r0f", a, b)], after=[gate["v"]])
+            if k in PRM["rv"][t]:
+                for x in range(a, b, FL):
+                    y = min(b, x + FL)
+                    op("v", ("plain", y - x), lambda k=k, x=x, y=y: g.vector.tensor_tensor(T.r0f[:, x:y], R(k, x, y), T[ro][:, Z + x:Z + y], A.subtract),
+                       [("R%d" % k, 0, 512), (ro, Z + x, Z + y)], [("r0f", x, y)])
                 into(k, 0, "r0f", 0, a, b, True, False, [gate["p"]])
                 continue
             if t:
-                op("s", plain(b - a), lambda k=k, a=a, b=b: g.scalar.activation(T.r0f[:, a:b], R(k), F.Copy), [("R%d" % k, 0, 512)], [("r0f", a, b)],
-                   after=[gate["f"]])
-            into(k, 0, "r0f", 0, a, b, True, False, [gate["p"]])
-            into(k, 128, ro, Z, a, b, False, False)
+                affine("s", lambda a=a, b=b: T.r0f[:, a:b], lambda k=k: R(k), 1.0, 0.0, ("plain", b - a), [("R%d" % k, 0, 512)], [("r0f", a, b)], [gate["fs"]])
+                into(k, 0, "r0f", 0, a, b, True, False, [gate["p"]])
+            into(k, 128, ro, Z, a, b, False, False, [gate["p"]])
+        PD = PRM["pd"][t]
         for j in range(4):
-            a, b, qn = 512 * j, 512 * j + 512, ("q1", "ps", "q0")[j % 3]
-            op("s", plain(512), lambda a=a, b=b, qn=qn: g.scalar.activation(T[qn][:], T[W][:, a:b], F.Identity, bias=M / 2, scale=-0.5),
-               [(W, a, b)], [(qn, 0, 512)], after=[gate["s"]])
-            op("v", plain(512), lambda a=a, b=b, qn=qn: g.vector.tensor_tensor(T[dp][:, a:b], T[qn][:], T[ro][:, Z + a:Z + b], A.add),
+            a, b, qn = 512 * j, 512 * j + 512, ("q2", "q0", "q1")[j % 3]
+            if a < PD:
+                affine("s", lambda a=a, b=b: T[dp][:, a:b], lambda a=a, b=b: T[W][:, a:b], -4.0, 0.0, ("plain", 512), [(W, a, b)], [(dp, a, b)], [gate["s"]])
+                continue
+            affine("s", lambda qn=qn: T[qn][:], lambda a=a, b=b: T[W][:, a:b], -4.0, 0.0, ("plain", 512), [(W, a, b)], [(qn, 0, 512)], [gate["s"]])
+            op("v", ("plain", 512), lambda a=a, b=b, qn=qn: g.vector.tensor_tensor(T[dp][:, a:b], T[qn][:], T[ro][:, Z + a:Z + b], A.add),
                [(qn, 0, 512), (ro, Z + a, Z + b)], [(dp, a, b)])
         dma("g" if t else "y", lambda: T.yp[:], lambda: T[dp][:], [(dp, 0, V), (W, V, WN)], [("yp", 0, V)], (1024 if t else 512) * V, t > 0)
+        if PD:
+            dma("g", lambda: T.yp[:, 0:PD], lambda: T[ro][:, Z:Z + PD], [(ro, Z, Z + PD), (W, V, WN)], [("yp", 0, PD)], 1024 * PD, True)
 
-        VV = PRM["vv"][t]
-        cuts = sorted(set([0, VV, V] + start + PRM["cuts"]))
+        cuts = sorted(set([0, V] + start + PRM["cuts"]))
         prev = {}
 
-        def gather(q, out, a, b, i, shift, plus=None):
+        def gather(q, out, a, b, i, plus=None):
             win = lambda: T[W][:, 0:WN].indirect(T.nbo[:, i * 128 + a // 16:i * 128 + b // 16])
             rd = [(W, 0, WN), ("nbo", 0, 512)]
-            if q == "s":
-                fn = lambda: g.scalar.activation(T[out][:, a:b], win(), F.Identity, bias=shift)
-            elif plus is None:
-                fn = lambda: g.vector.tensor_scalar(T[out][:, a:b], win(), shift, None, A.add)
+            if plus is None:
+                fn = lambda: g.scalar.activation(T[out][:, a:b], win(), F.Copy)
             else:
                 fn = lambda: g.vector.tensor_tensor(T[out][:, a:b], win(), T[plus][:, a:b], A.add)
                 rd = rd + [(plus, a, b)]
-            prev[q] = op(q, picked(b - a), fn, rd, [(out, a, b)], after=[prev[q]] if q in prev else [])
+            prev[q] = op(q, ("pick", b - a), fn, rd, [(out, a, b)], after=[prev[q]] if q in prev else [])
 
-        def store(k):
+        def close(k):
             _, x, y = banks[k]
-            q = "v" if k in PRM["vcp"] else "s"
-            fn = (lambda: g.vector.tensor_copy(T.r0f[:, x:y], R(k))) if q == "v" else (lambda: g.scalar.activation(T.r0f[:, x:y], R(k), F.Copy))
-            prev[q] = op(q, plain(y - x), fn, [("R%d" % k, 0, 512)], [("r0f", x, y)], after=[prev[q]])
-            dma("y", lambda: T.yr[:, x:y], lambda: T.r0f[:, x:y], [("r0f", x, y)], [("yr", x, y)], 512 * (y - x))
+            last = t == RO - 1
+            if k in PRM["add"][t]:
+                out, ww = (T.r0f[:, x:y], ("r0f", x, y)) if last else (R(k), ("R%d" % k, 0, 512))
+                op("v", ("plain", y - x), lambda: g.vector.tensor_tensor(out, R(k), T.ac1[:, x:y], A.add), [("R%d" % k, 0, 512), ("ac1", x, y)], [ww])
+            elif last:
+                affine("s", lambda: T.r0f[:, x:y], lambda: R(k), 1.0, 0.0, ("plain", y - x), [("R%d" % k, 0, 512)], [("r0f", x, y)])
+            if last:
+                dma("y", lambda: T.yr[:, x:y], lambda: T.r0f[:, x:y], [("r0f", x, y)], [("yr", x, y)], 512 * (y - x))
+            else:
+                steps_ab(t + 1, k, x, y)
 
         for a, b in zip(cuts[:-1], cuts[1:]):
             k = max(x for x in range(NB) if start[x] <= a)
             closing = b == start[k] + BANKS[k]
+            pieces = 1 if k in PRM["add"][t] else 2
             for i in range(2):
-                gather("v" if a < VV else "s", "pc%d" % i, a, b, 2 + i, -2 * M)
+                gather("s", "pc%d" % i, a, b, 2 + i)
             for i in range(2):
-                gather("v", "ac%d" % i, a, b, i, None, "pc%d" % i)
-                into(k, 256, "ac%d" % i, 0, a, b, False, closing and i == 1)
-            if closing and t < RO - 1:
-                steps_ab(t + 1, k, banks[k][1], banks[k][2])
-            elif closing:
-                for kk in ([k - 1] if k else []) + ([k] if k == NB - 1 else []):
-                    store(kk)
+                gather("v", "ac%d" % i, a, b, i, "pc%d" % i)
+                if i < pieces:
+                    into(k, 0, "ac%d" % i, 0, a, b, False, closing and i == pieces - 1)
+            if closing:
+                close(k)
 
     for t in range(RO):
         one_round(t)

@@ -7,27 +7,35 @@ WN = V + (N - 1) * G
 BIG = float(2 ** 23)
 K = 4096.0
 EIGHTH, DOWN = 0.125, -0.4375
+FL = 256
 PRM = {
     "banks": [512, 512, 512, 384, 128],
     "cuts": [128],
-    "early": 128,
-    "f": [256, 256],
-    "ev": 0,
-    "sv": [192, 192, 192],
-    "wv": [0, 0, 0],
-    "cv": [0, 1, 2, 3, 4],
-    "rv": [[], [0, 1, 2, 3, 4], [0, 1, 2, 3, 4]],
-    "add": [[], [], [1, 3, 4]],
-    "pd": [0, 0, 0],
-    "fill": 256,
-    "fac": 1.25, "gat": 1.56, "link": 1.6, "lat": 1.5, "issue": 0.6, "hop": 0.1, "look": 0.25, "dma": 300e3,
+    "chains": [[0], [1], [2]],
+    "calls": [([0, 1, 2], 0, CAP), ([0], CAP, G), ([1, 2], CAP, G)],
+    "f": [208, 0, 0],
+    "ev": 256,
+    "sv": [384, 192, 192],
+    "wv": [512, 512, 0],
+    "cg": [0],
+    "add": [1, 3, 4],
+    "pd": [1, 1, 0],
+    "soon": [0, 0, 0],
+    "pc": [1024],
+    "lag": [[3, 0, 3, 0], [3, 0, 3, 0], [3, 0, 2, 0]],
+    "V": ["f0 e h0 c0 o0 v0 h1 h2 c1 o1 c2 v1 o2 v2", "+ ro3 f0 ro4 e h0 c0 o0 v0 h1 h2 c1 o1 c2 v1 o2 v2", "+ ro3 f0 ro4 e h0 c0 o0 v0 h1 h2 c1 o1 c2 v1 o2 v2"],
+    "S": ["f0 e f1 f2 v0 + + v1 v2", "f0 e f1 f2 v0 + + v1 v2", "f0 e f1 f2 v0 + + v1 v2"],
+    "P": ["+ s0 t0 s1 s2 t1 t2", "s0 t0 s1 s2 t1 t2", "s0 t0 s1 s2 t1 t2"],
+    "late": [[0, 0], [0, 0], [2, 1]],
+    "pre": [0, 1, 1],
 }
+PRM.update({'banks': [512, 512, 512, 320, 192], 'cuts': [192], 'f': [160, 0, 0], 'ev': 384, 'sv': [256, 128, 192], 'wv': [512, 512, 256], 'cg': [0, 1], 'soon': [1, 1, 0], 'lag': [[5, 0, 5, 0], [5, 0, 5, 0], [3, 0, 2, 0]], 'V': ['e f0 + h0 c0 o0 v0 h1 h2 c1 o1 c2 v1 o2 v2', 'ro3 ro4 f0 e h0 + c0 o0 v0 h1 + h2 c1 o1 c2 o2 v1 v2', 'ro3 ro4 f0 e h0 + c0 o0 v0 h1 + h2 c1 o1 c2 o2 v1 v2'], 'S': ['f0 f1 f2 + v0 + + v1 v2', 'f0 f1 f2 v0 + + + v1 v2', 'f0 f1 f2 v0 + + + v1 v2'], 'late': [[0, 0], [0, 0], [1, 0]]})
 NB = len(PRM["banks"])
 
 SCRATCH = {}
 for _dt, _bufs in (("int32", (("r0i", V), ("thi", 4), ("nbi", 512), ("sni", 96))),
                    ("uint16", (("nbo", 512), ("sno", 96), ("sne", 24))),
-                   ("float32", (("r0f", V), ("bias", 4), ("sn8", 96), ("eye0", 256), ("eye", 256), ("rst", 96), ("cnt", 96), ("sel", 96),
+                   ("float32", (("r0f", V), ("bias", 4), ("sn8", 96), ("eye0", 256), ("eye", 256), ("rst", 96), ("cnt", 96),
                                 ("pc0", V), ("pc1", V), ("ac0", V), ("ac1", V))),
                    ("bfloat16", (("c1", 144), ("ck", 128), ("t1", 144), ("t2", 144), ("t3", 128), ("t4", 128), ("bw", 144), ("lo", 128),
                                  ("up", 128), ("hot", 96), ("fl", 3 * G), ("Y", V)))):
@@ -41,7 +49,7 @@ for _n in PSUM:
     SCRATCH[_n] = ("psum", [128, 512], "float32")
 
 NDMA = 32
-SEMAPHORES = ["cv", "cs", "cp", "cg"] + ["arr%d" % t for t in range(RO)] + ["snt%d" % k for k in range(3 * RO)] + \
+SEMAPHORES = ["cv", "cs", "cp", "cg"] + ["arr%d" % t for t in range(RO)] + ["snt%d" % k for k in range(5 * RO)] + \
              ["d%d" % k for k in range(NDMA)]
 
 
@@ -52,12 +60,10 @@ def split(engines, parts):
     return [engines[k * n:(k + 1) * n] for k in range(parts)]
 
 
-def engine_plan(topo, src, dsts):
+def engine_plan(topo, src, dsts, group):
     off = [d for d in dsts if topo.chip(d) != topo.chip(src)]
-    plan = {}
-    if off:
-        plan.update(zip(off, split(topo.engines(src, off[0]), len(off))))
-    far = [c for c in range(48) if topo.chip(c) != topo.chip(src) and topo.may_write(src, c)][0]
+    far = [c for c in group if topo.chip(c) != topo.chip(src)][0]
+    plan = dict(zip(off, split(topo.engines(src, far), len(off)))) if off else {}
     for d in dsts:
         if d not in off:
             plan[d] = split([e for e in topo.engines(src, d) if e not in topo.engines(src, far)], 1)[0]
@@ -66,334 +72,17 @@ def engine_plan(topo, src, dsts):
 
 def calls_of(topo, cores, rank):
     off = [j for j in range(N - 1) if topo.chip(cores[(rank + 1 + j) % N]) != topo.chip(cores[rank])]
-    first = 0 if 0 in off else N - 2
-    rest = sorted([j for j in range(N - 1) if j != first], key=lambda j: j not in off)
-    E = PRM["early"]
-    return ([([first] + rest, 0, E)] if E else []) + [([first], E, G), (rest, E, G)]
+    order = off + [j for j in range(N - 1) if j not in off]
+    if 0 not in off:
+        order[:2] = order[1::-1]
+    return order, [([order[i] for i in js], a, b) for js, a, b in PRM["calls"]]
 
 
-def hold_of(q, cost):
-    kind, n, f = cost[0], cost[1], PRM["fac"]
-    if kind == "plain":
-        return 0.055 + max(64, n) * 0.83e-3 * f
-    if kind == "pick":
-        return 0.06 + n * 0.83e-3 * f * PRM["gat"]
-    if kind == "pe":
-        return 0.015 + n * 0.417e-3 * f
-    if kind == "g":
-        return 0.17 + n * 1.66e-3 * f
-    if kind == "dma":
-        return 1.0 if q == "g" else 0.1
-    return PRM["issue"] if kind == "rem" else 0.0
-
-
-def schedule(ops):
-    hop, look = PRM["hop"], PRM["look"]
-    for o in ops:
-        o["next"] = []
-    for o in ops:
-        for d in o["order"]:
-            d["next"].append(o)
-    for o in reversed(ops):
-        o["tail"] = o["hold"] + o["lag"] + max([hop + x["tail"] for x in o["next"]] + [0.0])
-        o["left"] = len(o["order"])
-        o["ready"] = 0.0
-    free, lane = {}, {}
-    pool = [o for o in ops if o["left"] == 0]
-    while pool:
-        best = None
-        for q in sorted(set(o["q"] for o in pool)):
-            mine = [o for o in pool if o["q"] == q]
-            now = max(free.get(q, 0.0), min(o["ready"] for o in mine))
-            pick = max([o for o in mine if o["ready"] <= now + look], key=lambda o: (o["tail"], -o["n"]))
-            at = max(now, pick["ready"])
-            if best is None or (at, pick["n"]) < (best[0], best[1]["n"]):
-                best = (at, pick)
-        at, o = best
-        pool = [x for x in pool if x is not o]
-        o["at"] = at
-        free[o["q"]] = at + o["hold"]
-        done = at + o["hold"] + o["lag"]
-        if o["lane"]:
-            done = max(done, lane.get(o["lane"][0], 0.0) + o["lane"][1])
-            lane[o["lane"][0]] = done
-        for x in o["next"]:
-            x["ready"] = max(x["ready"], done + (hop if any(d is o for d in x["deps"]) else 0.0))
-            x["left"] -= 1
-            if x["left"] == 0:
-                pool.append(x)
-
-
-def rank_program(g, core, T, topo):
-    rank = T.rank_of(core)
-    if rank is None:
-        return
-    A, F = AluOpType, ActivationFunctionType
-    ops = []
+def issue(g, T, ops, lists):
     queue = {"v": g.vector, "s": g.scalar, "p": g.tensor, "g": g, "y": g.sync}
     counter = {"v": T.sem.cv, "s": T.sem.cs, "p": T.sem.cp, "g": T.sem.cg}
-    ndma = [0]
-
-    def op(q, cost, fn, reads, writes, kind="c", token=None, lag=0.0, lane=None, after=()):
-        deps = []
-        for o in ops:
-            hit = False
-            for mine, theirs, rr in ((writes, o["w"], 0), (writes, o["r"], 0), (reads, o["w"], 0), (reads, o["r"], 1)):
-                for (n, a, b) in mine:
-                    for (n2, a2, b2) in theirs:
-                        if n == n2 and ((n in PSUM and o["q"] != q) or (not rr and a < b2 and a2 < b)):
-                            hit = True
-            if hit:
-                deps.append(o)
-        if kind == "d":
-            token = (T.sem["d%d" % ndma[0]], 16, "d%d" % ndma[0])
-            ndma[0] += 1
-        o = {"q": q, "cost": cost, "hold": hold_of(q, cost), "lag": lag, "lane": lane, "fn": fn, "r": reads, "w": writes, "kind": kind,
-             "tok": token, "n": len(ops), "order": deps + list(after), "deps": [d for d in deps if not (d["q"] == "p" and q == "p")]}
-        ops.append(o)
-        return o
-
-    def dma(q, out, src, reads, writes, nbytes, add=False):
-        fn = (lambda: g.dma_start(out(), src(), accum_op=A.add)) if add else (lambda: queue[q].dma_start(out(), src()))
-        move = nbytes / PRM["dma"]
-        return op(q, ("dma", nbytes), fn, reads, writes, "d", lag=1.7 + move, lane=("local", move))
-
-    def affine(q, out, src, scale, shift, cost, reads, writes, after=()):
-        if q == "v":
-            fn = lambda: g.vector.tensor_scalar(out(), src(), scale, shift, A.mult, A.add)
-        else:
-            fn = lambda: g.scalar.activation(out(), src(), F.Identity, bias=shift, scale=scale)
-        return op(q, cost, fn, reads, writes, after=after)
-
-    BANKS = PRM["banks"]
-    start = [sum(BANKS[:k]) for k in range(NB)]
-    banks = [(k, start[k], start[k] + BANKS[k]) for k in range(NB)]
-    dsts = [T.cores[(rank + d) % N] for d in range(1, N)]
-    calls = calls_of(topo, T.cores, rank)
-    landing = 0
-    for d in range(1, N):
-        q = (rank - d) % N
-        for js, _, _ in calls_of(topo, T.cores, q):
-            landing += len(engine_plan(topo, T.cores[q], [T.cores[(q + 1 + j) % N] for j in js]).get(core, []))
-    E = PRM["early"]
-    (first,), rest = calls[-2][0], calls[-1][0]
-
-    def R(k, a=None, b=None):
-        if a is None:
-            return T["R%d" % k][:, 0:BANKS[k]]
-        return T["R%d" % k][:, a - start[k]:b - start[k]]
-
-    dma("s", lambda: T.thi[:, 0:1], lambda: T.th[:], [], [("thi", 0, 4)], 512)
-    for k, a, b in banks:
-        dma("y", lambda a=a, b=b: T.r0i[:, a:b], lambda a=a, b=b: T.r0[:, a:b], [], [("r0i", a, b)], 512 * (b - a))
-    dma("s", lambda: T.sni[:], lambda: T.snd[:], [], [("sni", 0, 96)], 512 * 96)
-    dma("y", lambda: T.nbi[:], lambda: T.nb[:], [("r0i", V - 1, V)], [("nbi", 0, 512)], 512 * 512)
-
-    def fill(name, a, b, val, step=1):
-        op("v", ("plain", b - a), lambda: g.vector.memset(T[name][:, a:b:step] if step > 1 else T[name][:, a:b], val), [], [(name, a, b)])
-
-    fill("c1", 0, 144, 1.0)
-    fill("eye0", 0, 128, 1.0)
-    fill("eye0", 128, 256, -1.0)
-    fill("ck", 0, 128, -K)
-    fill("rst", 0, 96, -1.0e9)
-    for t in range(RO):
-        fill("ro%d" % t, 0, Z, 0.0)
-    fill("rst", 0, 96, CAP * K, 32)
-
-    def sel(out, src, w, pattern, cmp, base, cm):
-        op("g", ("g", w), lambda: g.affine_select(T[out][:], T[src][:], pattern, cmp, 0.0, base, cm), [(src, 0, w)], [(out, 0, w)])
-
-    sel("eye", "eye0", 256, [[0, 2], [-1, 128]], A.is_equal, 0, 1)
-    sel("t1", "c1", 144, [[0, 9], [1, 16]], A.is_equal, -15, 0)
-    sel("t2", "t1", 144, [[1, 144]], A.is_ge, 0, -1)
-    sel("bw", "t2", 144, [[-1, 144]], A.is_ge, 15, 1)
-    sel("t3", "ck", 128, [[-16, 8], [0, 16]], A.is_ge, 0, 1)
-    sel("lo", "t3", 128, [[1, 128]], A.is_gt, 0, -1)
-    sel("t4", "ck", 128, [[16, 8], [0, 16]], A.is_ge, 15, -1)
-    sel("up", "t4", 128, [[-1, 128]], A.is_ge, 0, 1)
-
-    op("v", ("plain", 1), lambda: g.vector.tensor_scalar(T.bias[:, 0:1], T.thi[:, 0:1], -0.5, -BIG, A.add, A.mult), [("thi", 0, 4)], [("bias", 0, 4)])
-    op("v", ("plain", 96), lambda: g.vector.tensor_copy(T.sno[:], T.sni[:]), [("sni", 0, 96)], [("sno", 0, 96)])
-    op("v", ("plain", 96), lambda: g.vector.tensor_scalar(T.sn8[:], T.sni[:], float(Z), None, A.add), [("sni", 0, 96)], [("sn8", 0, 96)])
-    for j in range(N - 1 if E else 0):
-        c, w = j * E // 16, E // 16
-        op("v", ("plain", w), lambda j=j, c=c, w=w: g.vector.tensor_scalar(T.sne[:, c:c + w], T.sni[:, 32 * j:32 * j + w], float(Z), None, A.add),
-           [("sni", 0, 96)], [("sne", c, c + w)])
-
-    def into(k, eye, src, shift, a, b, begin, end, after=()):
-        op("p", ("pe", 4 * (b - a)), lambda: g.tensor.matmul(R(k, a, b), T.eye[:, eye:eye + 128], T[src][:, shift + a:shift + b], begin, end),
-           [("eye", 0, 256), (src, shift + a, shift + b)], [("R%d" % k, 0, 512)], after=after)
-
-    def steps_ab(t, k, a, b):
-        if t == 0:
-            qn = "q%d" % (k % 3)
-            r, rr, y, yy = T.r0i[:, a:b], ("r0i", a, b), T[qn][:, 0:b - a], (qn, 0, 512)
-        else:
-            r, rr, y, yy = R(k), ("R%d" % k, 0, 512), T.Y[:, a:b], ("Y", a, b)
-        op("s", ("plain", b - a), lambda: g.scalar.activation(y, r, F.Relu, bias=T.bias[:, 0:1], scale=BIG), [rr, ("bias", 0, 4)], [yy])
-        op("v", ("plain", b - a), lambda: g.vector.tensor_tensor(T["ro%d" % t][:, Z + a:Z + b], r, y, A.min), [rr, yy], [("ro%d" % t, Z + a, Z + b)])
-
-    for k, a, b in banks:
-        steps_ab(0, k, a, b)
-    for k, a, b in banks:
-        affine("v" if k in PRM["cv"] else "s", lambda a=a, b=b: T.r0f[:, a:b], lambda a=a, b=b: T.r0i[:, a:b], 1.0, 0.0, ("plain", b - a),
-               [("r0i", a, b)], [("r0f", a, b)])
-        into(k, 0, "r0f", 0, a, b, True, False)
-
-    def one_round(t):
-        ro, W, sb, of, dp = ("ro%d" % t, "W%d" % t, "sb%d" % t, "of%d" % t, "dp%d" % t)
-        gate = {}
-        over, shift = (ro, Z) if t == 0 else ("Y", 0)
-
-        def place(j, a):
-            return j * E + a if a < E else (N - 1) * E + j * (G - E) + a - E
-
-        def room(blocks, bank, fv):
-            s0, s1 = min(blocks) * G, (max(blocks) + 1) * G
-            sm, c0, c1, w = s0 + fv, s0 // 16, s1 // 16, (s1 - s0) // 16
-            for q, a, b in (("v", s0, sm), ("s", sm, s1)):
-                if a < b:
-                    gate["f" + q] = affine(q, lambda a=a, b=b: T.fl[:, a:b], lambda a=a, b=b: T[over][:, shift:shift + V].indirect(T.sno[:, a // 16:b // 16]),
-                                           1.0, 0.0, ("pick", b - a), [(over, shift, shift + V), ("sno", 0, 96)], [("fl", a, b)])
-
-            def seeds():
-                for i in range(16):
-                    ins = g.tensor.matmul(T[bank][:, 0:w], T.bw[:, 15 - i:143 - i], T.fl[:, s0 + i:s1:16], i == 0, i == 15)
-                return ins
-
-            def before():
-                g.tensor.matmul(T[bank][:, 128:128 + w], T.lo[:], T.hot[:, c0:c1], True, False)
-                for j in range(len(blocks)):
-                    ins = g.tensor.matmul(T[bank][:, 129 + 32 * j:160 + 32 * j], T.up[:], T.hot[:, c0 + 32 * j:c0 + 32 * j + 31],
-                                          False, j == len(blocks) - 1)
-                return ins
-
-            op("p", ("pe", 1100), seeds, [("bw", 0, 144), ("fl", s0, s1)], [(bank, 0, w)])
-            op("v", ("plain", w), lambda: g.vector.tensor_scalar(T.hot[:, c0:c1], T[bank][:, 0:w], 1.0, None, A.min), [(bank, 0, w)], [("hot", c0, c1)])
-            gate["p"] = op("p", ("pe", 192), before, [("lo", 0, 128), ("up", 0, 128), ("hot", c0, c1)], [(bank, 128, 128 + w)])
-            op("v", ("plain", w), lambda: g.vector.tensor_tensor_scan(T.cnt[:, c0:c1], T.rst[:, c0:c1], T[bank][:, 128:128 + w], 0.0, A.max, A.add),
-               [("rst", 0, 96), (bank, 128, 128 + w)], [("cnt", c0, c1)])
-            op("v", ("plain", 2 * w), lambda: g.vector.tensor_tensor(T.sel[:, c0:c1], T.cnt[:, c0:c1], T.sn8[:, c0:c1], A.min),
-               [("cnt", c0, c1), ("sn8", 0, 96)], [("sel", c0, c1)])
-            op("v", ("plain", w), lambda: g.vector.tensor_scalar(T[of][:, c0:c1], T.sel[:, c0:c1], 0.0, None, A.max), [("sel", c0, c1)], [(of, c0, c1)])
-
-        def values(tile, col, a, b, nv, after=()):
-            for q, x, y in (("v", a, a + nv), ("s", a + nv, b)):
-                if x < y:
-                    c0, c1 = col + (x - a) // 16, col + (y - a) // 16
-                    gate[q] = affine(q, lambda x=x, y=y: T[sb][:, x:y], lambda c0=c0, c1=c1: T[ro][:, 0:Z + V].indirect(T[tile][:, c0:c1]),
-                                     EIGHTH, DOWN, ("pick", y - x), [(ro, 0, Z + V), (tile, c0, c1)], [(sb, x, y)], after)
-
-        def send(n):
-            js, a, b = calls[n]
-            name = "snt%d" % (3 * t + n)
-            plan = engine_plan(topo, core, [dsts[j] for j in js])
-            units = sum(topo.chip(dsts[j]) != topo.chip(core) for j in js) * (b - a) / G
-
-            def fn():
-                trs = []
-                for j in js:
-                    rid, pid, _ = topo.addr(dsts[j])
-                    trs.append(RemoteDMATransfer(dst_ids=[DstId(rid=rid, pnc=pid)], dma_engine_mask=sum(1 << e for e in plan[dsts[j]]),
-                                                 remote_sem=T.sem["arr%d" % t], src=T[sb][:, place(j, a):place(j, a) + b - a],
-                                                 dst=T[W][:, V + j * G + a:V + j * G + b]))
-                return g.remote_dma_fused(trs, local_sem=T.sem[name])
-            return op("g", ("rem", units), fn, [(sb, place(j, a), place(j, a) + b - a) for j in js], [], "r",
-                      (T.sem[name], sum(len(plan[dsts[j]]) for j in js), name), PRM["lat"] + units * PRM["link"], ("link", units * PRM["link"]))
-
-        sends = []
-        room([first], "q0", PRM["f"][0])
-        if E:
-            values("sne", 0, 0, (N - 1) * E, PRM["ev"], [gate[x] for x in ("fv", "fs") if x in gate])
-            sends.append(send(0))
-        values(of, (first * G + E) // 16, place(first, E), place(first, E) + G - E, PRM["sv"][0])
-        sends.append(send(len(sends)))
-        room(rest, "q1", PRM["f"][1])
-        for n, j in enumerate(rest):
-            values(of, (j * G + E) // 16, place(j, E), place(j, E) + G - E, PRM["sv"][1 + n])
-        sends.append(send(len(sends)))
-        for x, y in zip(sends[:-1], sends[1:]):
-            y["order"].append(x)
-        op("x", ("x", 0), None, [], [(W, V, WN)], "x", (T.sem["arr%d" % t], landing, "arr%d" % t), after=sends)
-
-        if t == 0:
-            op("v", ("plain", 512), lambda: g.vector.tensor_copy(T.nbo[:], T.nbi[:]), [("nbi", 0, 512)], [("nbo", 0, 512)])
-        FL = PRM["fill"]
-        for a in range(0, V, FL):
-            affine("v" if a < PRM["wv"][t] else "s", lambda a=a: T[W][:, a:a + FL], lambda a=a: T[ro][:, Z + a:Z + a + FL], EIGHTH, DOWN, ("plain", FL),
-                   [(ro, Z + a, Z + a + FL)], [(W, a, a + FL)], [gate["fs"]])
-        for k, a, b in banks:
-            if k in PRM["rv"][t]:
-                for x in range(a, b, FL):
-                    y = min(b, x + FL)
-                    op("v", ("plain", y - x), lambda k=k, x=x, y=y: g.vector.tensor_tensor(T.r0f[:, x:y], R(k, x, y), T[ro][:, Z + x:Z + y], A.subtract),
-                       [("R%d" % k, 0, 512), (ro, Z + x, Z + y)], [("r0f", x, y)])
-                into(k, 0, "r0f", 0, a, b, True, False, [gate["p"]])
-                continue
-            if t:
-                affine("s", lambda a=a, b=b: T.r0f[:, a:b], lambda k=k: R(k), 1.0, 0.0, ("plain", b - a), [("R%d" % k, 0, 512)], [("r0f", a, b)], [gate["fs"]])
-                into(k, 0, "r0f", 0, a, b, True, False, [gate["p"]])
-            into(k, 128, ro, Z, a, b, False, False, [gate["p"]])
-        PD = PRM["pd"][t]
-        for j in range(4):
-            a, b, qn = 512 * j, 512 * j + 512, ("q2", "q0", "q1")[j % 3]
-            if a < PD:
-                affine("s", lambda a=a, b=b: T[dp][:, a:b], lambda a=a, b=b: T[W][:, a:b], -4.0, 0.0, ("plain", 512), [(W, a, b)], [(dp, a, b)], [gate["s"]])
-                continue
-            affine("s", lambda qn=qn: T[qn][:], lambda a=a, b=b: T[W][:, a:b], -4.0, 0.0, ("plain", 512), [(W, a, b)], [(qn, 0, 512)], [gate["s"]])
-            op("v", ("plain", 512), lambda a=a, b=b, qn=qn: g.vector.tensor_tensor(T[dp][:, a:b], T[qn][:], T[ro][:, Z + a:Z + b], A.add),
-               [(qn, 0, 512), (ro, Z + a, Z + b)], [(dp, a, b)])
-        dma("g" if t else "y", lambda: T.yp[:], lambda: T[dp][:], [(dp, 0, V), (W, V, WN)], [("yp", 0, V)], (1024 if t else 512) * V, t > 0)
-        if PD:
-            dma("g", lambda: T.yp[:, 0:PD], lambda: T[ro][:, Z:Z + PD], [(ro, Z, Z + PD), (W, V, WN)], [("yp", 0, PD)], 1024 * PD, True)
-
-        cuts = sorted(set([0, V] + start + PRM["cuts"]))
-        prev = {}
-
-        def gather(q, out, a, b, i, plus=None):
-            win = lambda: T[W][:, 0:WN].indirect(T.nbo[:, i * 128 + a // 16:i * 128 + b // 16])
-            rd = [(W, 0, WN), ("nbo", 0, 512)]
-            if plus is None:
-                fn = lambda: g.scalar.activation(T[out][:, a:b], win(), F.Copy)
-            else:
-                fn = lambda: g.vector.tensor_tensor(T[out][:, a:b], win(), T[plus][:, a:b], A.add)
-                rd = rd + [(plus, a, b)]
-            prev[q] = op(q, ("pick", b - a), fn, rd, [(out, a, b)], after=[prev[q]] if q in prev else [])
-
-        def close(k):
-            _, x, y = banks[k]
-            last = t == RO - 1
-            if k in PRM["add"][t]:
-                out, ww = (T.r0f[:, x:y], ("r0f", x, y)) if last else (R(k), ("R%d" % k, 0, 512))
-                op("v", ("plain", y - x), lambda: g.vector.tensor_tensor(out, R(k), T.ac1[:, x:y], A.add), [("R%d" % k, 0, 512), ("ac1", x, y)], [ww])
-            elif last:
-                affine("s", lambda: T.r0f[:, x:y], lambda: R(k), 1.0, 0.0, ("plain", y - x), [("R%d" % k, 0, 512)], [("r0f", x, y)])
-            if last:
-                dma("y", lambda: T.yr[:, x:y], lambda: T.r0f[:, x:y], [("r0f", x, y)], [("yr", x, y)], 512 * (y - x))
-            else:
-                steps_ab(t + 1, k, x, y)
-
-        for a, b in zip(cuts[:-1], cuts[1:]):
-            k = max(x for x in range(NB) if start[x] <= a)
-            closing = b == start[k] + BANKS[k]
-            pieces = 1 if k in PRM["add"][t] else 2
-            for i in range(2):
-                gather("s", "pc%d" % i, a, b, 2 + i)
-            for i in range(2):
-                gather("v", "ac%d" % i, a, b, i, "pc%d" % i)
-                if i < pieces:
-                    into(k, 0, "ac%d" % i, 0, a, b, False, closing and i == pieces - 1)
-            if closing:
-                close(k)
-
-    for t in range(RO):
-        one_round(t)
-
-    schedule(ops)
-    lists, total = {}, {}
+    total = {}
     for q in queue:
-        lists[q] = sorted([o for o in ops if o["q"] == q], key=lambda o: (o["at"], o["n"]))
         n = 0
         for o in lists[q]:
             if o["kind"] == "c":
@@ -411,7 +100,7 @@ def rank_program(g, core, T, topo):
             for name in need:
                 queue[q].wait_ge(need[name][0], need[name][1])
                 seen[name] = need[name][1]
-            ins = o["fn"]()
+            ins = o["fn"](queue[q])
             if o["kind"] == "c":
                 ins.then_inc(counter[q], 1)
             elif o["kind"] == "d":
@@ -421,3 +110,311 @@ def rank_program(g, core, T, topo):
     for o in ops:
         if o["kind"] in ("d", "r", "x"):
             g.wait_ge(o["tok"][0], o["tok"][1])
+
+
+def rank_program(g, core, T, topo):
+    rank = T.rank_of(core)
+    if rank is None:
+        return
+    A, F = AluOpType, ActivationFunctionType
+    ops = []
+    lists = {q: [] for q in "vspgyx"}
+    ndma = [0]
+
+    def op(q, cost, fn, reads, writes, kind="c", token=None):
+        deps = []
+        for o in ops:
+            hit = False
+            for mine, theirs, rr in ((writes, o["w"], 0), (writes, o["r"], 0), (reads, o["w"], 0), (reads, o["r"], 1)):
+                for (n, a, b) in mine:
+                    for (n2, a2, b2) in theirs:
+                        if n == n2 and ((n in PSUM and o["q"] != q) or (not rr and a < b2 and a2 < b)):
+                            hit = True
+            if hit and not (o["q"] == "p" and q == "p"):
+                deps.append(o)
+        if kind == "d":
+            token = (T.sem["d%d" % ndma[0]], 16, "d%d" % ndma[0])
+            ndma[0] += 1
+        o = {"q": q, "cost": cost, "fn": fn, "r": reads, "w": writes, "kind": kind, "tok": token, "deps": deps}
+        ops.append(o)
+        return o
+
+    def put(*some):
+        for o in some:
+            lists[o["q"]].append(o)
+
+    def dma(q, out, src, reads, writes, nbytes, add=False):
+        fn = (lambda e: e.dma_start(out(), src(), accum_op=A.add)) if add else (lambda e: e.dma_start(out(), src()))
+        return op(q, ("dma", nbytes, add), fn, reads, writes, "d")
+
+    def affine(q, out, src, scale, shift, cost, reads, writes):
+        if q == "v":
+            fn = lambda e: e.tensor_scalar(out(), src(), scale, shift, A.mult, A.add)
+        else:
+            fn = lambda e: e.activation(out(), src(), F.Identity, bias=shift, scale=scale)
+        return op(q, cost, fn, reads, writes)
+
+    BANKS = PRM["banks"]
+    start = [sum(BANKS[:k]) for k in range(NB)]
+    banks = [(k, start[k], start[k] + BANKS[k]) for k in range(NB)]
+    dsts = [T.cores[(rank + d) % N] for d in range(1, N)]
+    order, calls = calls_of(topo, T.cores, rank)
+    landing = 0
+    for d in range(1, N):
+        q = (rank - d) % N
+        for js, _, _ in calls_of(topo, T.cores, q)[1]:
+            landing += len(engine_plan(topo, T.cores[q], [T.cores[(q + 1 + j) % N] for j in js], T.cores).get(core, []))
+    early = calls[0][0] if calls[0][2] == CAP else []
+    place, n = {}, 0
+    for js, a, b in calls:
+        for j in js:
+            place[j, a] = n
+            n += b - a
+
+    def R(k, a=None, b=None):
+        if a is None:
+            return T["R%d" % k][:, 0:BANKS[k]]
+        return T["R%d" % k][:, a - start[k]:b - start[k]]
+
+    put(dma("s", lambda: T.thi[:, 0:1], lambda: T.th[:], [], [("thi", 0, 4)], 512))
+    put(dma("s", lambda: T.sni[:], lambda: T.snd[:], [], [("sni", 0, 96)], 512 * 96))
+    for k, a, b in banks:
+        put(dma("y", lambda a=a, b=b: T.r0i[:, a:b], lambda a=a, b=b: T.r0[:, a:b], [], [("r0i", a, b)], 512 * (b - a)))
+    put(dma("y", lambda: T.nbi[:], lambda: T.nb[:], [("r0i", V - 1, V)], [("nbi", 0, 512)], 512 * 512))
+
+    def fill(name, a, b, val, step=1):
+        put(op("v", ("plain", b - a), lambda e: e.memset(T[name][:, a:b:step] if step > 1 else T[name][:, a:b], val), [], [(name, a, b)]))
+
+    fill("eye0", 0, 128, 1.0)
+    fill("eye0", 128, 256, -1.0)
+    fill("c1", 0, 144, 1.0)
+    fill("ck", 0, 128, -K)
+    fill("rst", 0, 96, -1.0e9)
+    for t in range(RO):
+        fill("ro%d" % t, 0, Z, 0.0)
+    fill("rst", 0, 96, CAP * K, 32)
+
+    def sel(out, src, w, pattern, cmp, base, cm):
+        put(op("g", ("g", w), lambda e: e.affine_select(T[out][:], T[src][:], pattern, cmp, 0.0, base, cm), [(src, 0, w)], [(out, 0, w)]))
+
+    sel("eye", "eye0", 256, [[0, 2], [-1, 128]], A.is_equal, 0, 1)
+    sel("t1", "c1", 144, [[0, 9], [1, 16]], A.is_equal, -15, 0)
+    sel("t3", "ck", 128, [[-16, 8], [0, 16]], A.is_ge, 0, 1)
+    sel("t2", "t1", 144, [[1, 144]], A.is_ge, 0, -1)
+    sel("t4", "ck", 128, [[16, 8], [0, 16]], A.is_ge, 15, -1)
+    sel("bw", "t2", 144, [[-1, 144]], A.is_ge, 15, 1)
+    sel("lo", "t3", 128, [[1, 128]], A.is_gt, 0, -1)
+    sel("up", "t4", 128, [[-1, 128]], A.is_ge, 0, 1)
+
+    put(op("v", ("plain", 1), lambda e: e.tensor_scalar(T.bias[:, 0:1], T.thi[:, 0:1], -0.5, -BIG, A.add, A.mult), [("thi", 0, 4)], [("bias", 0, 4)]))
+    put(op("v", ("plain", 96), lambda e: e.tensor_copy(T.sno[:], T.sni[:]), [("sni", 0, 96)], [("sno", 0, 96)]))
+    put(op("v", ("plain", 96), lambda e: e.tensor_scalar(T.sn8[:], T.sni[:], float(Z), None, A.add), [("sni", 0, 96)], [("sn8", 0, 96)]))
+    for n, j in enumerate(early):
+        c, w = n * CAP // 16, CAP // 16
+        put(op("v", ("plain", w), lambda e, j=j, c=c, w=w: e.tensor_scalar(T.sne[:, c:c + w], T.sni[:, 32 * j:32 * j + w], float(Z), None, A.add),
+               [("sni", 0, 96)], [("sne", c, c + w)]))
+
+    def into(k, eye, src, shift, a, b, begin, end):
+        return op("p", ("pe", 4 * (b - a)), lambda e: e.matmul(R(k, a, b), T.eye[:, eye:eye + 128], T[src][:, shift + a:shift + b], begin, end),
+                  [("eye", 0, 256), (src, shift + a, shift + b)], [("R%d" % k, 0, 512)])
+
+    def steps_ab(t, k, a, b):
+        if t == 0:
+            qn = "q%d" % (k % 3)
+            r, rr, y, yy = T.r0i[:, a:b], ("r0i", a, b), T[qn][:, 0:b - a], (qn, 0, 512)
+        else:
+            r, rr, y, yy = R(k), ("R%d" % k, 0, 512), T.Y[:, a:b], ("Y", a, b)
+        return [op("s", ("plain", b - a), lambda e: e.activation(y, r, F.Relu, bias=T.bias[:, 0:1], scale=BIG), [rr, ("bias", 0, 4)], [yy]),
+                op("v", ("plain", b - a), lambda e: e.tensor_tensor(T["ro%d" % t][:, Z + a:Z + b], r, y, A.min), [rr, yy], [("ro%d" % t, Z + a, Z + b)])]
+
+    for k, a, b in banks:
+        put(*steps_ab(0, k, a, b))
+    opens0 = []
+    for k, a, b in banks:
+        if k in PRM["cg"]:
+            put(op("g", ("g", b - a), lambda e, a=a, b=b: e.affine_select(T.r0f[:, a:b], T.r0i[:, a:b], [[0, b - a]], A.is_ge, 0.0, 0, 0),
+                   [("r0i", a, b)], [("r0f", a, b)]))
+            opens0.append(into(k, 0, "r0f", 0, a, b, True, False))
+
+    def wait_phase(t, held):
+        ro, W, sb, of, dp = ("ro%d" % t, "W%d" % t, "sb%d" % t, "of%d" % t, "dp%d" % t)
+        over, shift = (ro, Z) if t == 0 else ("Y", 0)
+        tag = dict(held)
+        spare = {"v": [], "s": [], "p": list(opens0) if t == 0 else []}
+
+        def room(n, blocks, bank, fv):
+            s0, s1 = min(blocks) * G, (max(blocks) + 1) * G
+            sm, c0, c1, w = s0 + fv, s0 // 16, s1 // 16, (s1 - s0) // 16
+            for q, a, b in (("v", s0, sm), ("s", sm, s1)):
+                if a < b:
+                    tag[q, "f%d" % n] = affine(q, lambda a=a, b=b: T.fl[:, a:b],
+                                               lambda a=a, b=b: T[over][:, shift:shift + V].indirect(T.sno[:, a // 16:b // 16]),
+                                               1.0, 0.0, ("pick", b - a), [(over, shift, shift + V), ("sno", 0, 96)], [("fl", a, b)])
+
+            def seeds(e):
+                for i in range(16):
+                    ins = e.matmul(T[bank][:, 0:w], T.bw[:, 15 - i:143 - i], T.fl[:, s0 + i:s1:16], i == 0, i == 15)
+                return ins
+
+            def before(e):
+                e.matmul(T[bank][:, 128:128 + w], T.lo[:], T.hot[:, c0:c1], True, False)
+                for j in range(len(blocks)):
+                    ins = e.matmul(T[bank][:, 129 + 32 * j:160 + 32 * j], T.up[:], T.hot[:, c0 + 32 * j:c0 + 32 * j + 31], False, j == len(blocks) - 1)
+                return ins
+
+            tag["p", "s%d" % n] = op("p", ("pe", 16 * max(w, 64) + 80), seeds, [("bw", 0, 144), ("fl", s0, s1)], [(bank, 0, w)])
+            tag["v", "h%d" % n] = op("v", ("plain", w), lambda e: e.tensor_scalar(T.hot[:, c0:c1], T[bank][:, 0:w], 1.0, None, A.min),
+                                     [(bank, 0, w)], [("hot", c0, c1)])
+            tag["p", "t%d" % n] = op("p", ("pe", 192), before, [("lo", 0, 128), ("up", 0, 128), ("hot", c0, c1)], [(bank, 128, 128 + w)])
+            tag["v", "c%d" % n] = op("v", ("plain", w),
+                                     lambda e: e.tensor_tensor_scan(T.cnt[:, c0:c1], T.rst[:, c0:c1], T[bank][:, 128:128 + w], 0.0, A.max, A.add),
+                                     [("rst", 0, 96), (bank, 128, 128 + w)], [("cnt", c0, c1)])
+            tag["v", "o%d" % n] = op("v", ("plain", 2 * w), lambda e: e.tensor_tensor(T[of][:, c0:c1], T.cnt[:, c0:c1], T.sn8[:, c0:c1], A.min),
+                                     [("cnt", c0, c1), ("sn8", 0, 96)], [(of, c0, c1)])
+
+        def values(name, tile, col, a, b, nv):
+            for q, x, y in (("v", a, a + nv), ("s", a + nv, b)):
+                if x < y:
+                    c0, c1 = col + (x - a) // 16, col + (y - a) // 16
+                    tag[q, name] = affine(q, lambda x=x, y=y: T[sb][:, x:y], lambda c0=c0, c1=c1: T[ro][:, 0:Z + V].indirect(T[tile][:, c0:c1]),
+                                          EIGHTH, DOWN, ("pick", y - x), [(ro, 0, Z + V), (tile, c0, c1)], [(sb, x, y)])
+
+        def send(n):
+            js, a, b = calls[n]
+            name = "snt%d" % (5 * t + n)
+            plan = engine_plan(topo, core, [dsts[j] for j in js], T.cores)
+            units = sum(topo.chip(dsts[j]) != topo.chip(core) for j in js) * (b - a) / G
+
+            def fn(e):
+                trs = []
+                for j in js:
+                    rid, pid, _ = topo.addr(dsts[j])
+                    trs.append(RemoteDMATransfer(dst_ids=[DstId(rid=rid, pnc=pid)], dma_engine_mask=sum(1 << x for x in plan[dsts[j]]),
+                                                 remote_sem=T.sem["arr%d" % t], src=T[sb][:, place[j, a]:place[j, a] + b - a],
+                                                 dst=T[W][:, V + j * G + a:V + j * G + b]))
+                return e.remote_dma_fused(trs, local_sem=T.sem[name])
+            return op("g", ("rem", units, len(js) * (b - a) / G - units), fn, [(sb, place[j, a], place[j, a] + b - a) for j in js], [], "r",
+                      (T.sem[name], sum(len(plan[dsts[j]]) for j in js), name))
+
+        for n, part in enumerate(PRM["chains"]):
+            room(n, [order[i] for i in part], "q%d" % n, PRM["f"][n])
+        if early:
+            values("e", "sne", 0, 0, len(early) * CAP, PRM["ev"])
+        for js, a, b in calls[1 if early else 0:]:
+            for j in js:
+                values("v%d" % order.index(j), of, (j * G + a) // 16, place[j, a], place[j, a] + b - a, min(b - a, PRM["sv"][order.index(j)]))
+        sends = [send(n) for n in range(len(calls))]
+        put(*sends)
+        land = op("x", ("x", 0), None, [], [(W, V, WN)], "x", (T.sem["arr%d" % t], landing, "arr%d" % t))
+        land["sends"] = sends
+        put(land)
+
+        for k, a, b in banks:
+            if t == 0 and k in PRM["cg"]:
+                spare["p"].append(into(k, 128, ro, Z, a, b, False, False))
+                continue
+            for x in range(a, b, FL):
+                y = min(b, x + FL)
+                r, rr = (R(k, x, y), ("R%d" % k, 0, 512)) if t else (T.r0i[:, x:y], ("r0i", x, y))
+                spare["v"].append(op("v", ("plain", (y - x) * (1 if t else 2)),
+                                     lambda e, r=r, x=x, y=y: e.tensor_tensor(T.r0f[:, x:y], r, T[ro][:, Z + x:Z + y], A.subtract),
+                                     [rr, (ro, Z + x, Z + y)], [("r0f", x, y)]))
+            spare["p"].append(into(k, 0, "r0f", 0, a, b, True, False))
+        for a in range(0, 512 if t == 0 else 0, FL):
+            spare["v"].append(affine("v", lambda a=a: T.nbo[:, a:a + FL], lambda a=a: T.nbi[:, a:a + FL], 1.0, 0.0, ("plain", FL), [("nbi", 0, 512)],
+                                     [("nbo", a, a + FL)]))
+        for a in range(0, V, FL):
+            q = "v" if a >= V - PRM["wv"][t] else "s"
+            spare[q].append(affine(q, lambda a=a: T[W][:, a:a + FL], lambda a=a: T[ro][:, Z + a:Z + a + FL], EIGHTH, DOWN, ("plain", FL),
+                                   [(ro, Z + a, Z + a + FL)], [(W, a, a + FL)]))
+        PD = PRM["pd"][t]
+        for j in range(4):
+            a, b, qn = 512 * j, 512 * j + 512, "q%d" % (j % 3)
+            if PD:
+                spare["s"].append(affine("s", lambda a=a, b=b: T[dp][:, a:b], lambda a=a, b=b: T[W][:, a:b], -4.0, 0.0, ("plain", 512), [(W, a, b)], [(dp, a, b)]))
+                continue
+            spare["s"].append(affine("s", lambda qn=qn: T[qn][:], lambda a=a, b=b: T[W][:, a:b], -4.0, 0.0, ("plain", 512), [(W, a, b)], [(qn, 0, 512)]))
+            spare["v"].append(op("v", ("plain", 512), lambda e, a=a, b=b, qn=qn: e.tensor_tensor(T[dp][:, a:b], T[qn][:], T[ro][:, Z + a:Z + b], A.add),
+                                 [(qn, 0, 512), (ro, Z + a, Z + b)], [(dp, a, b)]))
+        if PD:
+            soon = PRM["soon"][t]
+            o = dma("g" if t else "y", lambda: T.yp[:], lambda: T[ro][:, Z:Z + V], [(ro, Z, Z + V)] + ([] if soon else [(W, V, WN)]),
+                    [("yp", 0, V)], 512 * V, t > 0)
+            if soon and t == 0:
+                o["deps"].append(sends[-1])
+            put(o)
+        pcuts = [0] + (PRM["pc"] if t == RO - 1 else []) + [V]
+        for a, b in zip(pcuts[:-1], pcuts[1:]):
+            add = t > 0 or PD > 0
+            put(dma("g" if add else "y", lambda a=a, b=b: T.yp[:, a:b], lambda a=a, b=b: T[dp][:, a:b], [(dp, a, b), (W, V, WN)], [("yp", a, b)],
+                    512 * (b - a), add))
+        for q in "vsp":
+            for name in PRM[q.upper()][t].split():
+                if name == "+":
+                    put(*spare[q][:1])
+                    del spare[q][:1]
+                elif (q, name) in tag:
+                    put(tag.pop((q, name)))
+            keep = len(spare[q]) - (PRM["late"][t]["vs".index(q)] if q != "p" else 0)
+            put(*spare[q][:keep])
+            del spare[q][:keep]
+        assert not tag, list(tag)
+        return spare
+
+    def sum_phase(t, spare):
+        W, last = "W%d" % t, t == RO - 1
+        cuts = sorted(set([0, V] + start + PRM["cuts"]))
+
+        def gather(q, out, a, b, i, plus=None):
+            win = lambda: T[W][:, 0:WN].indirect(T.nbo[:, i * 128 + a // 16:i * 128 + b // 16])
+            rd = [(W, 0, WN), ("nbo", 0, 512)]
+            if plus is None:
+                return op(q, ("pick", b - a), lambda e: e.activation(T[out][:, a:b], win(), F.Copy), rd, [(out, a, b)])
+            return op(q, ("pick", b - a), lambda e: e.tensor_tensor(T[out][:, a:b], win(), T[plus][:, a:b], A.add), rd + [(plus, a, b)], [(out, a, b)])
+
+        def close(k):
+            _, x, y = banks[k]
+            if not last:
+                return steps_ab(t + 1, k, x, y)
+            if k in PRM["add"]:
+                o = op("v", ("plain", y - x), lambda e: e.tensor_tensor(T.r0f[:, x:y], R(k), T.ac1[:, x:y], A.add), [("R%d" % k, 0, 512), ("ac1", x, y)],
+                       [("r0f", x, y)])
+            else:
+                o = affine("s", lambda: T.r0f[:, x:y], lambda: R(k), 1.0, 0.0, ("plain", y - x), [("R%d" % k, 0, 512)], [("r0f", x, y)])
+            return [o, dma("y", lambda: T.yr[:, x:y], lambda: T.r0f[:, x:y], [("r0f", x, y)], [("yr", x, y)], 512 * (y - x))]
+
+        due = {"s": [], "v": [], "y": []}
+        lag = {"s": 2 * PRM["lag"][t][0] + PRM["lag"][t][1], "v": 2 * PRM["lag"][t][2] + PRM["lag"][t][3], "y": 0}
+        put(*spare["v"][:1])
+        del spare["v"][:1]
+        for n, (a, b) in enumerate(zip(cuts[:-1], cuts[1:])):
+            k = max(x for x in range(NB) if start[x] <= a)
+            closing = b == start[k] + BANKS[k]
+            pieces = 1 if last and k in PRM["add"] else 2
+            for q in "sv":
+                for i in range(2):
+                    while due[q] and due[q][0][0] <= 2 * n + i:
+                        put(due[q].pop(0)[1])
+                    put(gather("s", "pc%d" % i, a, b, 2 + i) if q == "s" else gather("v", "ac%d" % i, a, b, i, "pc%d" % i))
+                    if q == "v" and i < pieces:
+                        put(into(k, 0, "ac%d" % i, 0, a, b, False, closing and i == pieces - 1))
+                if n < 2:
+                    put(*spare[q][:1])
+                    del spare[q][:1]
+            if closing:
+                for o in close(k):
+                    due[o["q"]].append((2 * n + lag[o["q"]], o))
+        put(*spare["v"])
+        put(*spare["s"])
+        held = {}
+        if not last:
+            held["v", "ro4"] = due["v"].pop()[1]
+            held["v", "ro3"] = due["v"].pop()[1]
+        for q in due:
+            put(*[o for _, o in due[q]])
+        return held
+
+    held = {}
+    for t in range(RO):
+        held = sum_phase(t, wait_phase(t, held))
+    issue(g, T, ops, lists)

@@ -8,37 +8,31 @@ BIG = float(2 ** 23)
 K = 4096.0
 EIGHTH, DOWN = 0.125, -0.4375
 FL = 256
-PRM = {
-    "banks": [512, 512, 512, 384, 128],
-    "cuts": [128],
-    "chains": [[0], [1], [2]],
-    "calls": [([0, 1, 2], 0, CAP), ([0], CAP, G), ([1, 2], CAP, G)],
-    "f": [208, 0, 0],
-    "ev": 256,
-    "sv": [384, 192, 192],
-    "wv": [512, 512, 0],
-    "cg": [0],
-    "add": [1, 3, 4],
-    "pd": [1, 1, 0],
-    "soon": [0, 0, 0],
-    "pc": [1024],
-    "lag": [[3, 0, 3, 0], [3, 0, 3, 0], [3, 0, 2, 0]],
-    "V": ["f0 e h0 c0 o0 v0 h1 h2 c1 o1 c2 v1 o2 v2", "+ ro3 f0 ro4 e h0 c0 o0 v0 h1 h2 c1 o1 c2 v1 o2 v2", "+ ro3 f0 ro4 e h0 c0 o0 v0 h1 h2 c1 o1 c2 v1 o2 v2"],
-    "S": ["f0 e f1 f2 v0 + + v1 v2", "f0 e f1 f2 v0 + + v1 v2", "f0 e f1 f2 v0 + + v1 v2"],
-    "P": ["+ s0 t0 s1 s2 t1 t2", "s0 t0 s1 s2 t1 t2", "s0 t0 s1 s2 t1 t2"],
-    "late": [[0, 0], [0, 0], [2, 1]],
-    "pre": [0, 1, 1],
-}
-PRM.update({'banks': [512, 512, 512, 320, 192], 'cuts': [192], 'f': [160, 0, 0], 'ev': 384, 'sv': [256, 128, 192], 'wv': [512, 512, 256], 'cg': [0, 1], 'soon': [1, 1, 0], 'lag': [[5, 0, 5, 0], [5, 0, 5, 0], [3, 0, 2, 0]], 'V': ['e f0 + h0 c0 o0 v0 h1 h2 c1 o1 c2 v1 o2 v2', 'ro3 ro4 f0 e h0 + c0 o0 v0 h1 + h2 c1 o1 c2 o2 v1 v2', 'ro3 ro4 f0 e h0 + c0 o0 v0 h1 + h2 c1 o1 c2 o2 v1 v2'], 'S': ['f0 f1 f2 + v0 + + v1 v2', 'f0 f1 f2 v0 + + + v1 v2', 'f0 f1 f2 v0 + + + v1 v2'], 'late': [[0, 0], [0, 0], [1, 0]]})
-NB = len(PRM["banks"])
+BANKS = [512, 512, 512, 384, 128]
+CHUNKS = [0, 192, 512, 1024, 1536, 1920]
+LOADS = [0, 512, 1024, 1408, 1728, 1920, 2048]
+STAGE = ["q0", "q1", "q2", "R3", "R2", "q0"]
+COUNTS = [[0], [1, 2]]
+CALLS = [([0, 1, 2], 0, CAP), ([0], CAP, G), ([1, 2], CAP, G)]
+FLAGS_V = [[0, 256], [0, 256], [0, 256]]
+LATE_V = [128, G - CAP, 0]
+S_V = [640, 384, 256]
+S_SHORT = [3, 2, 2]
+CAST_G = 2
+ADD_V = [[2], [2], [1, 3]]
+ORDER = {"v": ["e f1 h0 n8 c0 o0 h1 v0 c1 o1 v1 z1 z2"] + 2 * ["ro3 ro4 e h0 f1 c0 o0 + v0 h1 + c1 o1 v1"],
+         "s": ["f0 f1 + v0 + v2"] + 2 * ["Y3 Y4 f0 f1 + v0 + v2"],
+         "p": ["+ s0 t0 s1 t1"] + 2 * ["s0 t0 s1 t1"],
+         "g": ["x0 x1 x2 nb l8 u8 p0", "x0 x1 x2 ro p0", "x0 x1 x2 p0 p1"]}
+NB = len(BANKS)
 
-SCRATCH = {}
-for _dt, _bufs in (("int32", (("r0i", V), ("thi", 4), ("nbi", 512), ("sni", 96))),
+SCRATCH = {"sni": ("sbuf", [128, N - 1, G // 16], "int32")}
+for _dt, _bufs in (("int32", (("r0i", V), ("thi", 4), ("nbi", 512))),
                    ("uint16", (("nbo", 512), ("sno", 96), ("sne", 24))),
                    ("float32", (("r0f", V), ("bias", 4), ("sn8", 96), ("eye0", 256), ("eye", 256), ("rst", 96), ("cnt", 96),
                                 ("pc0", V), ("pc1", V), ("ac0", V), ("ac1", V))),
-                   ("bfloat16", (("c1", 144), ("ck", 128), ("t1", 144), ("t2", 144), ("t3", 128), ("t4", 128), ("bw", 144), ("lo", 128),
-                                 ("up", 128), ("hot", 96), ("fl", 3 * G), ("Y", V)))):
+                   ("bfloat16", (("ck", 128), ("t1", 144), ("t2", 144), ("t3", 128), ("t4", 128), ("bw", 144), ("lo", 128), ("up", 128),
+                                 ("lo8", 128), ("up8", 128), ("hot", 96), ("hot2", 64), ("fl", 3 * G), ("Y", V)))):
     for _n, _w in _bufs:
         SCRATCH[_n] = ("sbuf", [128, _w], _dt)
 for _t in range(RO):
@@ -48,8 +42,8 @@ PSUM = ["q0", "q1", "q2"] + ["R%d" % _k for _k in range(NB)]
 for _n in PSUM:
     SCRATCH[_n] = ("psum", [128, 512], "float32")
 
-NDMA = 32
-SEMAPHORES = ["cv", "cs", "cp", "cg"] + ["arr%d" % t for t in range(RO)] + ["snt%d" % k for k in range(5 * RO)] + \
+NDMA = 24
+SEMAPHORES = ["cv", "cs", "cp", "cg"] + ["arr%d" % t for t in range(RO)] + ["snt%d" % k for k in range(len(CALLS) * RO)] + \
              ["d%d" % k for k in range(NDMA)]
 
 
@@ -75,7 +69,7 @@ def calls_of(topo, cores, rank):
     order = off + [j for j in range(N - 1) if j not in off]
     if 0 not in off:
         order[:2] = order[1::-1]
-    return order, [([order[i] for i in js], a, b) for js, a, b in PRM["calls"]]
+    return order, [([order[i] for i in js], a, b) for js, a, b in CALLS]
 
 
 def issue(g, T, ops, lists):
@@ -89,27 +83,35 @@ def issue(g, T, ops, lists):
                 n += 1
                 o["tok"] = (counter[q], n, q)
         total[q] = n
+    for o in lists["x"]:
+        o["known"] = {}
+    seen, at = {q: {} for q in queue}, {q: 0 for q in queue}
+    while any(at[q] < len(lists[q]) for q in queue):
+        for q in queue:
+            while at[q] < len(lists[q]) and all("known" in d for d in lists[q][at[q]]["deps"]):
+                o, know = lists[q][at[q]], seen[q]
+                left = [d for d in o["deps"] if d["tok"][1] > know.get(d["tok"][2], 0)]
+                left = [d for d in left if not any(x["known"].get(d["tok"][2], 0) >= d["tok"][1]
+                                                   or (x["tok"][2] == d["tok"][2] and x["tok"][1] > d["tok"][1]) for x in left)]
+                o["waits"] = [d["tok"] for d in left]
+                for d in left:
+                    for name, val in list(d["known"].items()) + [(d["tok"][2], d["tok"][1])]:
+                        know[name] = max(know.get(name, 0), val)
+                o["known"] = dict(know)
+                at[q] += 1
     for q in queue:
-        seen = {}
         for o in lists[q]:
-            need = {}
-            for d in o["deps"]:
-                sem, val, name = d["tok"]
-                if val > seen.get(name, 0) and val > need.get(name, (None, 0))[1]:
-                    need[name] = (sem, val)
-            for name in need:
-                queue[q].wait_ge(need[name][0], need[name][1])
-                seen[name] = need[name][1]
+            for sem, val, _ in o["waits"]:
+                queue[q].wait_ge(sem, val)
             ins = o["fn"](queue[q])
             if o["kind"] == "c":
                 ins.then_inc(counter[q], 1)
             elif o["kind"] == "d":
                 ins.then_inc(o["tok"][0], 16)
-    for q in counter:
-        g.wait_ge(counter[q], total[q])
-    for o in ops:
-        if o["kind"] in ("d", "r", "x"):
-            g.wait_ge(o["tok"][0], o["tok"][1])
+    waited = set((name, val) for q in queue for o in lists[q] for _, val, name in o["waits"])
+    for sem, val, name in [o["tok"] for o in ops if o["kind"] != "c"] + [(counter[q], total[q], q) for q in counter]:
+        if (name, val) not in waited:
+            g.wait_ge(sem, val)
 
 
 def rank_program(g, core, T, topo):
@@ -117,44 +119,50 @@ def rank_program(g, core, T, topo):
     if rank is None:
         return
     A, F = AluOpType, ActivationFunctionType
-    ops = []
+    ops, touched, ndma = [], {}, [0]
     lists = {q: [] for q in "vspgyx"}
-    ndma = [0]
 
-    def op(q, cost, fn, reads, writes, kind="c", token=None):
-        deps = []
-        for o in ops:
-            hit = False
-            for mine, theirs, rr in ((writes, o["w"], 0), (writes, o["r"], 0), (reads, o["w"], 0), (reads, o["r"], 1)):
-                for (n, a, b) in mine:
-                    for (n2, a2, b2) in theirs:
-                        if n == n2 and ((n in PSUM and o["q"] != q) or (not rr and a < b2 and a2 < b)):
-                            hit = True
-            if hit and not (o["q"] == "p" and q == "p"):
-                deps.append(o)
+    def op(q, fn, reads, writes, kind="c", token=None):
+        touch = [(x, False) for x in reads] + [(x, True) for x in writes]
+        deps = {}
+        for (name, a, b), wr in touch:
+            for o, a2, b2, wr2 in touched.get(name, []):
+                if ((name in PSUM and o["q"] != q) or ((wr or wr2) and a < b2 and a2 < b)) and not (o["q"] == "p" and q == "p"):
+                    deps[o["n"]] = o
         if kind == "d":
             token = (T.sem["d%d" % ndma[0]], 16, "d%d" % ndma[0])
             ndma[0] += 1
-        o = {"q": q, "cost": cost, "fn": fn, "r": reads, "w": writes, "kind": kind, "tok": token, "deps": deps}
+        o = {"q": q, "fn": fn, "w": writes, "kind": kind, "tok": token, "deps": [deps[n] for n in sorted(deps)], "n": len(ops)}
         ops.append(o)
+        for (name, a, b), wr in touch:
+            touched.setdefault(name, []).append((o, a, b, wr))
         return o
 
     def put(*some):
         for o in some:
             lists[o["q"]].append(o)
 
-    def dma(q, out, src, reads, writes, nbytes, add=False):
-        fn = (lambda e: e.dma_start(out(), src(), accum_op=A.add)) if add else (lambda e: e.dma_start(out(), src()))
-        return op(q, ("dma", nbytes, add), fn, reads, writes, "d")
+    def dma(q, out, src, reads, writes, add=False):
+        fn = (lambda e: e.dma_start(out, src, accum_op=A.add)) if add else (lambda e: e.dma_start(out, src))
+        return op(q, fn, reads, writes, "d")
 
-    def affine(q, out, src, scale, shift, cost, reads, writes):
+    def affine(q, out, src, scale, shift, reads, writes):
         if q == "v":
-            fn = lambda e: e.tensor_scalar(out(), src(), scale, shift, A.mult, A.add)
-        else:
-            fn = lambda e: e.activation(out(), src(), F.Identity, bias=shift, scale=scale)
-        return op(q, cost, fn, reads, writes)
+            return op(q, lambda e: e.tensor_scalar(out, src, scale, shift, A.mult, A.add), reads, writes)
+        return op(q, lambda e: e.activation(out, src, F.Identity, bias=shift, scale=scale), reads, writes)
 
-    BANKS = PRM["banks"]
+    def pair(out, x, y, how, reads, writes):
+        return op("v", lambda e: e.tensor_tensor(out, x, y, how), reads, writes)
+
+    def fill(name, a, b, val, step=1):
+        return op("v", lambda e: e.memset(T[name][:, a:b:step] if step > 1 else T[name][:, a:b], val), [], [(name, a, b)])
+
+    def pick(out, src, a, b, pattern, cmp, base, cm):
+        return op("g", lambda e: e.affine_select(T[out][:, a:b], T[src][:, a:b], pattern, cmp, 0.0, base, cm), [(src, a, b)], [(out, a, b)])
+
+    def cast(out, src, a, b):
+        return pick(out, src, a, b, [[0, b - a]], A.is_ge, 0, 0)
+
     start = [sum(BANKS[:k]) for k in range(NB)]
     banks = [(k, start[k], start[k] + BANKS[k]) for k in range(NB)]
     dsts = [T.cores[(rank + d) % N] for d in range(1, N)]
@@ -164,257 +172,226 @@ def rank_program(g, core, T, topo):
         q = (rank - d) % N
         for js, _, _ in calls_of(topo, T.cores, q)[1]:
             landing += len(engine_plan(topo, T.cores[q], [T.cores[(q + 1 + j) % N] for j in js], T.cores).get(core, []))
-    early = calls[0][0] if calls[0][2] == CAP else []
     place, n = {}, 0
     for js, a, b in calls:
-        for j in js:
+        for j in sorted(js):
             place[j, a] = n
             n += b - a
 
-    def R(k, a=None, b=None):
-        if a is None:
-            return T["R%d" % k][:, 0:BANKS[k]]
+    def R(k, a, b):
         return T["R%d" % k][:, a - start[k]:b - start[k]]
 
-    put(dma("s", lambda: T.thi[:, 0:1], lambda: T.th[:], [], [("thi", 0, 4)], 512))
-    put(dma("s", lambda: T.sni[:], lambda: T.snd[:], [], [("sni", 0, 96)], 512 * 96))
-    for k, a, b in banks:
-        put(dma("y", lambda a=a, b=b: T.r0i[:, a:b], lambda a=a, b=b: T.r0[:, a:b], [], [("r0i", a, b)], 512 * (b - a)))
-    put(dma("y", lambda: T.nbi[:], lambda: T.nb[:], [("r0i", V - 1, V)], [("nbi", 0, 512)], 512 * 512))
-
-    def fill(name, a, b, val, step=1):
-        put(op("v", ("plain", b - a), lambda e: e.memset(T[name][:, a:b:step] if step > 1 else T[name][:, a:b], val), [], [(name, a, b)]))
-
-    fill("eye0", 0, 128, 1.0)
-    fill("eye0", 128, 256, -1.0)
-    fill("c1", 0, 144, 1.0)
-    fill("ck", 0, 128, -K)
-    fill("rst", 0, 96, -1.0e9)
-    for t in range(RO):
-        fill("ro%d" % t, 0, Z, 0.0)
-    fill("rst", 0, 96, CAP * K, 32)
-
-    def sel(out, src, w, pattern, cmp, base, cm):
-        put(op("g", ("g", w), lambda e: e.affine_select(T[out][:], T[src][:], pattern, cmp, 0.0, base, cm), [(src, 0, w)], [(out, 0, w)]))
-
-    sel("eye", "eye0", 256, [[0, 2], [-1, 128]], A.is_equal, 0, 1)
-    sel("t1", "c1", 144, [[0, 9], [1, 16]], A.is_equal, -15, 0)
-    sel("t3", "ck", 128, [[-16, 8], [0, 16]], A.is_ge, 0, 1)
-    sel("t2", "t1", 144, [[1, 144]], A.is_ge, 0, -1)
-    sel("t4", "ck", 128, [[16, 8], [0, 16]], A.is_ge, 15, -1)
-    sel("bw", "t2", 144, [[-1, 144]], A.is_ge, 15, 1)
-    sel("lo", "t3", 128, [[1, 128]], A.is_gt, 0, -1)
-    sel("up", "t4", 128, [[-1, 128]], A.is_ge, 0, 1)
-
-    put(op("v", ("plain", 1), lambda e: e.tensor_scalar(T.bias[:, 0:1], T.thi[:, 0:1], -0.5, -BIG, A.add, A.mult), [("thi", 0, 4)], [("bias", 0, 4)]))
-    put(op("v", ("plain", 96), lambda e: e.tensor_copy(T.sno[:], T.sni[:]), [("sni", 0, 96)], [("sno", 0, 96)]))
-    put(op("v", ("plain", 96), lambda e: e.tensor_scalar(T.sn8[:], T.sni[:], float(Z), None, A.add), [("sni", 0, 96)], [("sn8", 0, 96)]))
-    for n, j in enumerate(early):
-        c, w = n * CAP // 16, CAP // 16
-        put(op("v", ("plain", w), lambda e, j=j, c=c, w=w: e.tensor_scalar(T.sne[:, c:c + w], T.sni[:, 32 * j:32 * j + w], float(Z), None, A.add),
-               [("sni", 0, 96)], [("sne", c, c + w)]))
+    def bank(k):
+        return ("R%d" % k, 0, 512)
 
     def into(k, eye, src, shift, a, b, begin, end):
-        return op("p", ("pe", 4 * (b - a)), lambda e: e.matmul(R(k, a, b), T.eye[:, eye:eye + 128], T[src][:, shift + a:shift + b], begin, end),
-                  [("eye", 0, 256), (src, shift + a, shift + b)], [("R%d" % k, 0, 512)])
+        return op("p", lambda e: e.matmul(R(k, a, b), T.eye[:, eye:eye + 128], T[src][:, shift + a:shift + b], begin, end),
+                  [("eye", 0, 256), (src, shift + a, shift + b)], [bank(k)])
 
-    def steps_ab(t, k, a, b):
+    def thresholds(t, k, a, b):
         if t == 0:
-            qn = "q%d" % (k % 3)
-            r, rr, y, yy = T.r0i[:, a:b], ("r0i", a, b), T[qn][:, 0:b - a], (qn, 0, 512)
+            r, rr, y, yy = T.r0i[:, a:b], ("r0i", a, b), T[STAGE[k]][:, 0:b - a], (STAGE[k], 0, 512)
         else:
-            r, rr, y, yy = R(k), ("R%d" % k, 0, 512), T.Y[:, a:b], ("Y", a, b)
-        return [op("s", ("plain", b - a), lambda e: e.activation(y, r, F.Relu, bias=T.bias[:, 0:1], scale=BIG), [rr, ("bias", 0, 4)], [yy]),
-                op("v", ("plain", b - a), lambda e: e.tensor_tensor(T["ro%d" % t][:, Z + a:Z + b], r, y, A.min), [rr, yy], [("ro%d" % t, Z + a, Z + b)])]
+            r, rr, y, yy = R(k, a, b), bank(k), T.Y[:, a:b], ("Y", a, b)
+        return [op("s", lambda e: e.activation(y, r, F.Relu, bias=T.bias[:, 0:1], scale=BIG), [rr, ("bias", 0, 1)], [yy]),
+                pair(T["ro%d" % t][:, Z + a:Z + b], r, y, A.min, [rr, yy], [("ro%d" % t, Z + a, Z + b)])]
 
-    for k, a, b in banks:
-        put(*steps_ab(0, k, a, b))
-    opens0 = []
-    for k, a, b in banks:
-        if k in PRM["cg"]:
-            put(op("g", ("g", b - a), lambda e, a=a, b=b: e.affine_select(T.r0f[:, a:b], T.r0i[:, a:b], [[0, b - a]], A.is_ge, 0.0, 0, 0),
-                   [("r0i", a, b)], [("r0f", a, b)]))
-            opens0.append(into(k, 0, "r0f", 0, a, b, True, False))
+    put(dma("s", T.thi[:, 0:1], T.th[:], [], [("thi", 0, 4)]), dma("s", T.sni[:], T.snd[:], [], [("sni", 0, 96)]))
+    loads = list(zip(LOADS[:-1], LOADS[1:]))
+    for a, b in loads:
+        put(dma("y", T.r0i[:, a:b], T.r0[:, a:b], [], [("r0i", a, b)]))
+    put(dma("y", T.nbi[:], T.nb[:], [("r0i", V - 1, V)], [("nbi", 0, 512)]))
+    put(fill("eye0", 0, 128, 1.0), fill("eye0", 128, 256, -1.0), fill("t1", 0, 144, 0.0), fill("ck", 0, 128, -K), fill("t1", 15, 144, 1.0, 16),
+        fill("rst", 0, 96, -1.0e9),
+        op("v", lambda e: e.tensor_scalar(T.bias[:, 0:1], T.thi[:, 0:1], -0.5, -BIG, A.add, A.mult), [("thi", 0, 4)], [("bias", 0, 1)]),
+        fill("ro0", 0, Z, 0.0), fill("rst", 0, 96, CAP * K, 32),
+        op("v", lambda e: e.tensor_copy(T.bias[:, 1:2], T.thi[:, 0:1]), [("thi", 0, 4)], [("bias", 1, 2)]),
+        op("v", lambda e: e.tensor_copy(T.sno[:], T.sni[:]), [("sni", 0, 96)], [("sno", 0, 96)]),
+        op("v", lambda e: e.tensor_copy(T.sne[:], T.sni[:, :, 0:CAP // 16]), [("sni", 0, 96)], [("sne", 0, 24)]))
+    put(pick("eye", "eye0", 0, 256, [[0, 2], [-1, 128]], A.is_equal, 0, 1),
+        pick("t3", "ck", 0, 128, [[-16, 8], [0, 16]], A.is_ge, 0, 1),
+        pick("t2", "t1", 0, 144, [[1, 144]], A.is_ge, 0, -1),
+        pick("t4", "ck", 0, 128, [[16, 8], [0, 16]], A.is_ge, 15, -1),
+        cast("r0f", "r0i", banks[0][1], banks[0][2]),
+        pick("bw", "t2", 0, 144, [[-1, 144]], A.is_ge, 15, 1),
+        pick("lo", "t3", 0, 128, [[1, 128]], A.is_gt, 0, -1),
+        pick("up", "t4", 0, 128, [[-1, 128]], A.is_ge, 0, 1))
+    put(*[cast("r0f", "r0i", a, b) for _, a, b in banks[1:CAST_G]])
+    held = {("v", "n8"): affine("v", T.sn8[:], T.sni[:], 1.0, float(Z), [("sni", 0, 96)], [("sn8", 0, 96)])}
+    for t in range(1, RO):
+        held["v", "z%d" % t] = fill("ro%d" % t, 0, Z, 0.0)
+    for k, (a, b) in enumerate(loads):
+        put(*thresholds(0, k, a, b))
+    first_opens = [into(k, 0, "r0f", 0, a, b, True, False) for k, a, b in banks[:CAST_G]]
 
-    def wait_phase(t, held):
+    def under_way(t, named):
         ro, W, sb, of, dp = ("ro%d" % t, "W%d" % t, "sb%d" % t, "of%d" % t, "dp%d" % t)
-        over, shift = (ro, Z) if t == 0 else ("Y", 0)
-        tag = dict(held)
-        spare = {"v": [], "s": [], "p": list(opens0) if t == 0 else []}
+        last = t == RO - 1
+        spare = {"v": [], "s": [], "p": list(first_opens) if t == 0 else [], "g": []}
 
-        def room(n, blocks, bank, fv):
-            s0, s1 = min(blocks) * G, (max(blocks) + 1) * G
-            sm, c0, c1, w = s0 + fv, s0 // 16, s1 // 16, (s1 - s0) // 16
+        def count(n, blocks):
+            s0, s1, qn = min(blocks) * G, (max(blocks) + 1) * G, "q%d" % n
+            sm, c0, c1, w = s0 + FLAGS_V[t][n], s0 // 16, s1 // 16, (s1 - s0) // 16
             for q, a, b in (("v", s0, sm), ("s", sm, s1)):
-                if a < b:
-                    tag[q, "f%d" % n] = affine(q, lambda a=a, b=b: T.fl[:, a:b],
-                                               lambda a=a, b=b: T[over][:, shift:shift + V].indirect(T.sno[:, a // 16:b // 16]),
-                                               1.0, 0.0, ("pick", b - a), [(over, shift, shift + V), ("sno", 0, 96)], [("fl", a, b)])
+                if a == b:
+                    continue
+                src = "Y" if t else "r0i"
+                win, out = T[src][:, 0:V].indirect(T.sno[:, a // 16:b // 16]), T.fl[:, a:b]
+                rd, wr = [(src, 0, V), ("sno", 0, 96)], [("fl", a, b)]
+                if t:
+                    o = affine(q, out, win, 1.0, 0.0, rd, wr)
+                elif q == "s":
+                    o = op(q, lambda e, out=out, win=win: e.activation(out, win, F.Relu, bias=T.bias[:, 0:1], scale=BIG), rd + [("bias", 0, 4)], wr)
+                else:
+                    o = op(q, lambda e, out=out, win=win: e.tensor_scalar(out, win, T.bias[:, 1:2], None, A.is_ge), rd + [("bias", 0, 4)], wr)
+                named[q, "f%d" % n] = o
+            step = 8 if t and w == 32 else 16
+            hot, h0, hw = ("hot2", 0, 64) if step == 8 else ("hot", c0, w)
 
             def seeds(e):
-                for i in range(16):
-                    ins = e.matmul(T[bank][:, 0:w], T.bw[:, 15 - i:143 - i], T.fl[:, s0 + i:s1:16], i == 0, i == 15)
+                for i in range(step):
+                    ins = e.matmul(T[qn][:, 0:hw], T.bw[:, 15 - i:143 - i], T.fl[:, s0 + i:s1:step], i == 0, i == step - 1)
                 return ins
 
             def before(e):
-                e.matmul(T[bank][:, 128:128 + w], T.lo[:], T.hot[:, c0:c1], True, False)
-                for j in range(len(blocks)):
-                    ins = e.matmul(T[bank][:, 129 + 32 * j:160 + 32 * j], T.up[:], T.hot[:, c0 + 32 * j:c0 + 32 * j + 31], False, j == len(blocks) - 1)
+                if step == 8:
+                    runs = [(128, "lo", T.hot2[:, 0:64:2], 32), (128, "lo8", T.hot2[:, 1:64:2], 32),
+                            (129, "up", T.hot2[:, 0:62:2], 31), (129, "up8", T.hot2[:, 1:62:2], 31)]
+                else:
+                    runs = [(128, "lo", T.hot[:, c0:c1], w)] + [(129 + x, "up", T.hot[:, c0 + x:c0 + x + 31], 31) for x in range(0, w, 32)]
+                for i, (x, tri, rhs, m) in enumerate(runs):
+                    ins = e.matmul(T[qn][:, x:x + m], T[tri][:], rhs, i == 0, i == len(runs) - 1)
                 return ins
 
-            tag["p", "s%d" % n] = op("p", ("pe", 16 * max(w, 64) + 80), seeds, [("bw", 0, 144), ("fl", s0, s1)], [(bank, 0, w)])
-            tag["v", "h%d" % n] = op("v", ("plain", w), lambda e: e.tensor_scalar(T.hot[:, c0:c1], T[bank][:, 0:w], 1.0, None, A.min),
-                                     [(bank, 0, w)], [("hot", c0, c1)])
-            tag["p", "t%d" % n] = op("p", ("pe", 192), before, [("lo", 0, 128), ("up", 0, 128), ("hot", c0, c1)], [(bank, 128, 128 + w)])
-            tag["v", "c%d" % n] = op("v", ("plain", w),
-                                     lambda e: e.tensor_tensor_scan(T.cnt[:, c0:c1], T.rst[:, c0:c1], T[bank][:, 128:128 + w], 0.0, A.max, A.add),
-                                     [("rst", 0, 96), (bank, 128, 128 + w)], [("cnt", c0, c1)])
-            tag["v", "o%d" % n] = op("v", ("plain", 2 * w), lambda e: e.tensor_tensor(T[of][:, c0:c1], T.cnt[:, c0:c1], T.sn8[:, c0:c1], A.min),
-                                     [("cnt", c0, c1), ("sn8", 0, 96)], [(of, c0, c1)])
+            tris = [(x, 0, 128) for x in (("lo", "up", "lo8", "up8") if step == 8 else ("lo", "up"))]
+            named["p", "s%d" % n] = op("p", seeds, [("bw", 0, 144), ("fl", s0, s1)], [(qn, 0, hw)])
+            named["v", "h%d" % n] = op("v", lambda e: e.tensor_scalar(T[hot][:, h0:h0 + hw], T[qn][:, 0:hw], 1.0, None, A.min),
+                                       [(qn, 0, hw)], [(hot, h0, h0 + hw)])
+            named["p", "t%d" % n] = op("p", before, tris + [(hot, h0, h0 + hw)], [(qn, 128, 128 + w)])
+            named["v", "c%d" % n] = op("v", lambda e: e.tensor_tensor_scan(T.cnt[:, c0:c1], T.rst[:, c0:c1], T[qn][:, 128:128 + w], 0.0, A.max, A.add),
+                                       [("rst", 0, 96), (qn, 128, 128 + w)], [("cnt", c0, c1)])
+            named["v", "o%d" % n] = pair(T[of][:, c0:c1], T.cnt[:, c0:c1], T.sn8[:, c0:c1], A.min, [("cnt", c0, c1), ("sn8", 0, 96)], [(of, c0, c1)])
 
-        def values(name, tile, col, a, b, nv):
+        def values(name, tile, base, col, a, b, nv):
             for q, x, y in (("v", a, a + nv), ("s", a + nv, b)):
                 if x < y:
                     c0, c1 = col + (x - a) // 16, col + (y - a) // 16
-                    tag[q, name] = affine(q, lambda x=x, y=y: T[sb][:, x:y], lambda c0=c0, c1=c1: T[ro][:, 0:Z + V].indirect(T[tile][:, c0:c1]),
-                                          EIGHTH, DOWN, ("pick", y - x), [(ro, 0, Z + V), (tile, c0, c1)], [(sb, x, y)])
+                    named[q, name] = affine(q, T[sb][:, x:y], T[ro][:, base:Z + V].indirect(T[tile][:, c0:c1]), EIGHTH, DOWN,
+                                            [(ro, 0, Z + V), (tile, c0, c1)], [(sb, x, y)])
 
         def send(n):
             js, a, b = calls[n]
-            name = "snt%d" % (5 * t + n)
+            name = "snt%d" % (len(calls) * t + n)
             plan = engine_plan(topo, core, [dsts[j] for j in js], T.cores)
-            units = sum(topo.chip(dsts[j]) != topo.chip(core) for j in js) * (b - a) / G
-
-            def fn(e):
-                trs = []
-                for j in js:
-                    rid, pid, _ = topo.addr(dsts[j])
-                    trs.append(RemoteDMATransfer(dst_ids=[DstId(rid=rid, pnc=pid)], dma_engine_mask=sum(1 << x for x in plan[dsts[j]]),
-                                                 remote_sem=T.sem["arr%d" % t], src=T[sb][:, place[j, a]:place[j, a] + b - a],
-                                                 dst=T[W][:, V + j * G + a:V + j * G + b]))
-                return e.remote_dma_fused(trs, local_sem=T.sem[name])
-            return op("g", ("rem", units, len(js) * (b - a) / G - units), fn, [(sb, place[j, a], place[j, a] + b - a) for j in js], [], "r",
+            trs = []
+            for j in js:
+                rid, pid, _ = topo.addr(dsts[j])
+                trs.append(RemoteDMATransfer(dst_ids=[DstId(rid=rid, pnc=pid)], dma_engine_mask=sum(1 << x for x in plan[dsts[j]]),
+                                             remote_sem=T.sem["arr%d" % t], src=T[sb][:, place[j, a]:place[j, a] + b - a],
+                                             dst=T[W][:, V + j * G + a:V + j * G + b]))
+            return op("g", lambda e: e.remote_dma_fused(trs, local_sem=T.sem[name]), [(sb, place[j, a], place[j, a] + b - a) for j in js], [], "r",
                       (T.sem[name], sum(len(plan[dsts[j]]) for j in js), name))
 
-        for n, part in enumerate(PRM["chains"]):
-            room(n, [order[i] for i in part], "q%d" % n, PRM["f"][n])
-        if early:
-            values("e", "sne", 0, 0, len(early) * CAP, PRM["ev"])
-        for js, a, b in calls[1 if early else 0:]:
-            for j in js:
-                values("v%d" % order.index(j), of, (j * G + a) // 16, place[j, a], place[j, a] + b - a, min(b - a, PRM["sv"][order.index(j)]))
+        for n, part in enumerate(COUNTS):
+            count(n, [order[i] for i in part])
+        values("e", "sne", Z, 0, 0, (N - 1) * CAP, (N - 1) * CAP)
+        for i, j in enumerate(order):
+            values("v%d" % i, of, 0, (j * G + CAP) // 16, place[j, CAP], place[j, CAP] + G - CAP, LATE_V[i])
         sends = [send(n) for n in range(len(calls))]
-        put(*sends)
-        land = op("x", ("x", 0), None, [], [(W, V, WN)], "x", (T.sem["arr%d" % t], landing, "arr%d" % t))
-        land["sends"] = sends
-        put(land)
+        for n, o in enumerate(sends):
+            named["g", "x%d" % n] = o
+        put(op("x", None, [], [(W, V, WN)], "x", (T.sem["arr%d" % t], landing, "arr%d" % t)))
 
         for k, a, b in banks:
-            if t == 0 and k in PRM["cg"]:
+            if t == 0 and k < CAST_G:
                 spare["p"].append(into(k, 128, ro, Z, a, b, False, False))
                 continue
-            for x in range(a, b, FL):
-                y = min(b, x + FL)
-                r, rr = (R(k, x, y), ("R%d" % k, 0, 512)) if t else (T.r0i[:, x:y], ("r0i", x, y))
-                spare["v"].append(op("v", ("plain", (y - x) * (1 if t else 2)),
-                                     lambda e, r=r, x=x, y=y: e.tensor_tensor(T.r0f[:, x:y], r, T[ro][:, Z + x:Z + y], A.subtract),
-                                     [rr, (ro, Z + x, Z + y)], [("r0f", x, y)]))
-            spare["p"].append(into(k, 0, "r0f", 0, a, b, True, False))
-        for a in range(0, 512 if t == 0 else 0, FL):
-            spare["v"].append(affine("v", lambda a=a: T.nbo[:, a:a + FL], lambda a=a: T.nbi[:, a:a + FL], 1.0, 0.0, ("plain", FL), [("nbi", 0, 512)],
-                                     [("nbo", a, a + FL)]))
-        for a in range(0, V, FL):
-            q = "v" if a >= V - PRM["wv"][t] else "s"
-            spare[q].append(affine(q, lambda a=a: T[W][:, a:a + FL], lambda a=a: T[ro][:, Z + a:Z + a + FL], EIGHTH, DOWN, ("plain", FL),
-                                   [(ro, Z + a, Z + a + FL)], [(W, a, a + FL)]))
-        PD = PRM["pd"][t]
-        for j in range(4):
-            a, b, qn = 512 * j, 512 * j + 512, "q%d" % (j % 3)
-            if PD:
-                spare["s"].append(affine("s", lambda a=a, b=b: T[dp][:, a:b], lambda a=a, b=b: T[W][:, a:b], -4.0, 0.0, ("plain", 512), [(W, a, b)], [(dp, a, b)]))
-                continue
-            spare["s"].append(affine("s", lambda qn=qn: T[qn][:], lambda a=a, b=b: T[W][:, a:b], -4.0, 0.0, ("plain", 512), [(W, a, b)], [(qn, 0, 512)]))
-            spare["v"].append(op("v", ("plain", 512), lambda e, a=a, b=b, qn=qn: e.tensor_tensor(T[dp][:, a:b], T[qn][:], T[ro][:, Z + a:Z + b], A.add),
-                                 [(qn, 0, 512), (ro, Z + a, Z + b)], [(dp, a, b)]))
-        if PD:
-            soon = PRM["soon"][t]
-            o = dma("g" if t else "y", lambda: T.yp[:], lambda: T[ro][:, Z:Z + V], [(ro, Z, Z + V)] + ([] if soon else [(W, V, WN)]),
-                    [("yp", 0, V)], 512 * V, t > 0)
-            if soon and t == 0:
-                o["deps"].append(sends[-1])
-            put(o)
-        pcuts = [0] + (PRM["pc"] if t == RO - 1 else []) + [V]
-        for a, b in zip(pcuts[:-1], pcuts[1:]):
-            add = t > 0 or PD > 0
-            put(dma("g" if add else "y", lambda a=a, b=b: T.yp[:, a:b], lambda a=a, b=b: T[dp][:, a:b], [(dp, a, b), (W, V, WN)], [("yp", a, b)],
-                    512 * (b - a), add))
-        for q in "vsp":
-            for name in PRM[q.upper()][t].split():
-                if name == "+":
-                    put(*spare[q][:1])
-                    del spare[q][:1]
-                elif (q, name) in tag:
-                    put(tag.pop((q, name)))
-            keep = len(spare[q]) - (PRM["late"][t]["vs".index(q)] if q != "p" else 0)
-            put(*spare[q][:keep])
-            del spare[q][:keep]
-        assert not tag, list(tag)
-        return spare
+            w = FL if t == 0 or k == 0 else 512
+            for x in range(a, b, w):
+                y = min(b, x + w)
+                r, rr = (R(k, x, y), bank(k)) if t else (T.r0i[:, x:y], ("r0i", x, y))
+                spare["v"].append(pair(T.r0f[:, x:y], r, T[ro][:, Z + x:Z + y], A.subtract, [rr, (ro, Z + x, Z + y)], [("r0f", x, y)]))
+            if k < NB - 1:
+                spare["p"].append(into(k, 0, "r0f", 0, a, b, True, False))
+        if t == 0:
+            named["g", "l8"] = pick("lo8", "t3", 0, 128, [[1, 128]], A.is_gt, -8, -1)
+            named["g", "u8"] = pick("up8", "t4", 0, 128, [[-1, 128]], A.is_ge, 8, 1)
+            named["g", "nb"] = cast("nbo", "nbi", 0, 512)
+        cuts = list(range(0, FL * S_SHORT[t] + 1, FL)) + [V - S_V[t], V]
+        for a, b in zip(cuts[:-1], cuts[1:]):
+            q = "v" if b == V else "s"
+            spare[q].append(affine(q, T[W][:, a:b], T[ro][:, Z + a:Z + b], EIGHTH, DOWN, [(ro, Z + a, Z + b)], [(W, a, b)]))
+        for a in range(0, V, 512):
+            b, qn = a + 512, "q%d" % (a // 512 % 3)
+            if last:
+                spare["s"].append(affine("s", T[qn][:], T[W][:, a:b], -4.0, 0.0, [(W, a, b)], [(qn, 0, 512)]))
+                spare["v"].append(pair(T[dp][:, a:b], T[qn][:], T[ro][:, Z + a:Z + b], A.add, [(qn, 0, 512), (ro, Z + a, Z + b)], [(dp, a, b)]))
+            else:
+                q = "v" if b == V else "s"
+                spare[q].append(affine(q, T[dp][:, a:b], T[W][:, a:b], -4.0, 0.0, [(W, a, b)], [(dp, a, b)]))
+        if not last:
+            o = dma("g" if t else "y", T.yp[:], T[ro][:, Z:Z + V], [(ro, Z, Z + V)], [("yp", 0, V)], t > 0)
+            o["deps"].append(sends[-1])
+            if t:
+                named["g", "ro"] = o
+            else:
+                put(o)
+        for n, (a, b) in enumerate([(V // 2, V), (0, V // 2)] if last else [(0, V)]):
+            named["g", "p%d" % n] = dma("g", T.yp[:, a:b], T[dp][:, a:b], [(dp, a, b), (W, V, WN)], [("yp", a, b)], True)
+        for q in ORDER:
+            for name in ORDER[q][t].split():
+                put(spare[q].pop(0) if name == "+" else named.pop((q, name)))
+            put(*spare[q])
 
-    def sum_phase(t, spare):
+    def sums(t):
         W, last = "W%d" % t, t == RO - 1
-        cuts = sorted(set([0, V] + start + PRM["cuts"]))
 
-        def gather(q, out, a, b, i, plus=None):
-            win = lambda: T[W][:, 0:WN].indirect(T.nbo[:, i * 128 + a // 16:i * 128 + b // 16])
-            rd = [(W, 0, WN), ("nbo", 0, 512)]
+        def gather(out, a, b, i, plus=None):
+            win, rd = T[W][:, 0:WN].indirect(T.nbo[:, i * 128 + a // 16:i * 128 + b // 16]), [(W, 0, WN), ("nbo", 0, 512)]
             if plus is None:
-                return op(q, ("pick", b - a), lambda e: e.activation(T[out][:, a:b], win(), F.Copy), rd, [(out, a, b)])
-            return op(q, ("pick", b - a), lambda e: e.tensor_tensor(T[out][:, a:b], win(), T[plus][:, a:b], A.add), rd + [(plus, a, b)], [(out, a, b)])
+                return op("s", lambda e: e.activation(T[out][:, a:b], win, F.Copy), rd, [(out, a, b)])
+            return pair(T[out][:, a:b], win, T[plus][:, a:b], A.add, rd + [(plus, a, b)], [(out, a, b)])
 
         def close(k):
             _, x, y = banks[k]
-            if not last:
-                return steps_ab(t + 1, k, x, y)
-            if k in PRM["add"]:
-                o = op("v", ("plain", y - x), lambda e: e.tensor_tensor(T.r0f[:, x:y], R(k), T.ac1[:, x:y], A.add), [("R%d" % k, 0, 512), ("ac1", x, y)],
-                       [("r0f", x, y)])
-            else:
-                o = affine("s", lambda: T.r0f[:, x:y], lambda: R(k), 1.0, 0.0, ("plain", y - x), [("R%d" % k, 0, 512)], [("r0f", x, y)])
-            return [o, dma("y", lambda: T.yr[:, x:y], lambda: T.r0f[:, x:y], [("r0f", x, y)], [("yr", x, y)], 512 * (y - x))]
+            out, wr = (T.r0f[:, x:y], ("r0f", x, y)) if last else (R(k, x, y), bank(k))
+            some = []
+            if k in ADD_V[t]:
+                some.append(pair(out, R(k, x, y), T.ac1[:, x:y], A.add, [bank(k), ("ac1", x, y)], [wr]))
+            elif last:
+                some.append(affine("s", out, R(k, x, y), 1.0, 0.0, [bank(k)], [wr]))
+            if last:
+                return some + [dma("s" if k == NB - 1 else "y", T.yr[:, x:y], out, [wr], [("yr", x, y)])]
+            return some + thresholds(t + 1, k, x, y)
 
-        due = {"s": [], "v": [], "y": []}
-        lag = {"s": 2 * PRM["lag"][t][0] + PRM["lag"][t][1], "v": 2 * PRM["lag"][t][2] + PRM["lag"][t][3], "y": 0}
-        put(*spare["v"][:1])
-        del spare["v"][:1]
-        for n, (a, b) in enumerate(zip(cuts[:-1], cuts[1:])):
-            k = max(x for x in range(NB) if start[x] <= a)
-            closing = b == start[k] + BANKS[k]
-            pieces = 1 if last and k in PRM["add"] else 2
-            for q in "sv":
-                for i in range(2):
-                    while due[q] and due[q][0][0] <= 2 * n + i:
-                        put(due[q].pop(0)[1])
-                    put(gather("s", "pc%d" % i, a, b, 2 + i) if q == "s" else gather("v", "ac%d" % i, a, b, i, "pc%d" % i))
-                    if q == "v" and i < pieces:
-                        put(into(k, 0, "ac%d" % i, 0, a, b, False, closing and i == pieces - 1))
-                if n < 2:
-                    put(*spare[q][:1])
-                    del spare[q][:1]
+        k, x, y = banks[NB - 1]
+        put(gather("ac0", x, y, 0, "r0f"), gather("pc1", x, y, 1, "ac0"), into(k, 0, "pc1", 0, x, y, True, False))
+        after = []
+        for a, b in zip(CHUNKS[:-1], CHUNKS[1:]):
+            k = max(j for j in range(NB) if start[j] <= a)
+            if last and b == x:
+                put(*after[:4])
+                del after[:4]
+            pieces, closing = 1 if k in ADD_V[t] else 2, b == start[k] + BANKS[k]
+            put(gather("pc0", a, b, 2), gather("pc1", a, b, 3))
+            for i in range(2):
+                put(gather("ac%d" % i, a, b, i, "pc%d" % i))
+                if i < pieces:
+                    put(into(k, 0, "ac%d" % i, 0, a, b, False, closing and i == pieces - 1))
             if closing:
-                for o in close(k):
-                    due[o["q"]].append((2 * n + lag[o["q"]], o))
-        put(*spare["v"])
-        put(*spare["s"])
-        held = {}
-        if not last:
-            held["v", "ro4"] = due["v"].pop()[1]
-            held["v", "ro3"] = due["v"].pop()[1]
-        for q in due:
-            put(*[o for _, o in due[q]])
-        return held
+                after += close(k)
+        k = NB - 1
+        put(gather("pc0", x, y, 2), into(k, 0, "pc0", 0, x, y, False, False), gather("ac1", x, y, 3), into(k, 0, "ac1", 0, x, y, False, True))
+        after += close(k)
+        if last:
+            put(*after)
+            return {}
+        adds = [o for o in after if o["w"][0][0] in PSUM]
+        rest = [o for o in after if o["w"][0][0] not in PSUM]
+        put(*(adds + rest[:-4]))
+        return {("s", "Y3"): rest[-4], ("v", "ro3"): rest[-3], ("s", "Y4"): rest[-2], ("v", "ro4"): rest[-1]}
 
-    held = {}
     for t in range(RO):
-        held = sum_phase(t, wait_phase(t, held))
+        under_way(t, held)
+        held = sums(t)
     issue(g, T, ops, lists)

from concourse.bass import DstId, RemoteDMATransfer
from concourse.mybir import AluOpType, ActivationFunctionType

N, V, G, CAP, RO = 4, 2048, 512, 128, 3
Z = 8
WN = V + (N - 1) * G
BIG = float(2 ** 23)
K = 4096.0
EIGHTH, DOWN = 0.125, -0.4375
FL = 256
BANKS = [512, 512, 512, 384, 128]
CHUNKS = [0, 192, 512, 1024, 1536, 1920]
LOADS = [0, 512, 1024, 1408, 1728, 1920, 2048]
STAGE = ["q0", "q1", "q2", "R3", "R2", "q0"]
COUNTS = [[0], [1, 2]]
CALLS = [([0, 1, 2], 0, CAP), ([0], CAP, G), ([1, 2], CAP, G)]
FLAGS_V = [[0, 256], [0, 256], [0, 256]]
LATE_V = [128, G - CAP, 0]
S_V = [640, 384, 256]
S_SHORT = [3, 2, 2]
CAST_G = 2
ADD_V = [[2], [2], [1, 3]]
ORDER = {"v": ["e f1 h0 n8 c0 o0 h1 v0 c1 o1 v1 z1 z2"] + 2 * ["ro3 ro4 e h0 f1 c0 o0 + v0 h1 + c1 o1 v1"],
         "s": ["f0 f1 + v0 + v2"] + 2 * ["Y3 Y4 f0 f1 + v0 + v2"],
         "p": ["+ s0 t0 s1 t1"] + 2 * ["s0 t0 s1 t1"],
         "g": ["x0 x1 x2 nb l8 u8 p0", "x0 x1 x2 ro p0", "x0 x1 x2 p0 p1"]}
NB = len(BANKS)

SCRATCH = {"sni": ("sbuf", [128, N - 1, G // 16], "int32")}
for _dt, _bufs in (("int32", (("r0i", V), ("thi", 4), ("nbi", 512))),
                   ("uint16", (("nbo", 512), ("sno", 96), ("sne", 24))),
                   ("float32", (("r0f", V), ("bias", 4), ("sn8", 96), ("eye0", 256), ("eye", 256), ("rst", 96), ("cnt", 96),
                                ("pc0", V), ("pc1", V), ("ac0", V), ("ac1", V))),
                   ("bfloat16", (("ck", 128), ("t1", 144), ("t2", 144), ("t3", 128), ("t4", 128), ("bw", 144), ("lo", 128), ("up", 128),
                                 ("lo8", 128), ("up8", 128), ("hot", 96), ("hot2", 64), ("fl", 3 * G), ("Y", V)))):
    for _n, _w in _bufs:
        SCRATCH[_n] = ("sbuf", [128, _w], _dt)
for _t in range(RO):
    for _n, _w, _dt in (("ro", Z + V, "float32"), ("W", WN, "int32"), ("sb", 3 * G, "int32"), ("of", 96, "uint16"), ("dp", V, "float32")):
        SCRATCH["%s%d" % (_n, _t)] = ("sbuf", [128, _w], _dt)
PSUM = ["q0", "q1", "q2"] + ["R%d" % _k for _k in range(NB)]
for _n in PSUM:
    SCRATCH[_n] = ("psum", [128, 512], "float32")

NDMA = 24
SEMAPHORES = ["cv", "cs", "cp", "cg"] + ["arr%d" % t for t in range(RO)] + ["snt%d" % k for k in range(len(CALLS) * RO)] + \
             ["d%d" % k for k in range(NDMA)]


def split(engines, parts):
    n = 1
    while 2 * n * parts <= len(engines):
        n *= 2
    return [engines[k * n:(k + 1) * n] for k in range(parts)]


def engine_plan(topo, src, dsts, group):
    off = [d for d in dsts if topo.chip(d) != topo.chip(src)]
    far = [c for c in group if topo.chip(c) != topo.chip(src)][0]
    plan = dict(zip(off, split(topo.engines(src, far), len(off)))) if off else {}
    for d in dsts:
        if d not in off:
            plan[d] = split([e for e in topo.engines(src, d) if e not in topo.engines(src, far)], 1)[0]
    return plan


def calls_of(topo, cores, rank):
    off = [j for j in range(N - 1) if topo.chip(cores[(rank + 1 + j) % N]) != topo.chip(cores[rank])]
    order = off + [j for j in range(N - 1) if j not in off]
    if 0 not in off:
        order[:2] = order[1::-1]
    return order, [([order[i] for i in js], a, b) for js, a, b in CALLS]


def issue(g, T, ops, lists):
    queue = {"v": g.vector, "s": g.scalar, "p": g.tensor, "g": g, "y": g.sync}
    counter = {"v": T.sem.cv, "s": T.sem.cs, "p": T.sem.cp, "g": T.sem.cg}
    total = {}
    for q in queue:
        n = 0
        for o in lists[q]:
            if o["kind"] == "c":
                n += 1
                o["tok"] = (counter[q], n, q)
        total[q] = n
    for o in lists["x"]:
        o["known"] = {}
    seen, at = {q: {} for q in queue}, {q: 0 for q in queue}
    while any(at[q] < len(lists[q]) for q in queue):
        for q in queue:
            while at[q] < len(lists[q]) and all("known" in d for d in lists[q][at[q]]["deps"]):
                o, know = lists[q][at[q]], seen[q]
                left = [d for d in o["deps"] if d["tok"][1] > know.get(d["tok"][2], 0)]
                left = [d for d in left if not any(x["known"].get(d["tok"][2], 0) >= d["tok"][1]
                                                   or (x["tok"][2] == d["tok"][2] and x["tok"][1] > d["tok"][1]) for x in left)]
                o["waits"] = [d["tok"] for d in left]
                for d in left:
                    for name, val in list(d["known"].items()) + [(d["tok"][2], d["tok"][1])]:
                        know[name] = max(know.get(name, 0), val)
                o["known"] = dict(know)
                at[q] += 1
    for q in queue:
        for o in lists[q]:
            for sem, val, _ in o["waits"]:
                queue[q].wait_ge(sem, val)
            ins = o["fn"](queue[q])
            if o["kind"] == "c":
                ins.then_inc(counter[q], 1)
            elif o["kind"] == "d":
                ins.then_inc(o["tok"][0], 16)
    waited = set((name, val) for q in queue for o in lists[q] for _, val, name in o["waits"])
    for sem, val, name in [o["tok"] for o in ops if o["kind"] != "c"] + [(counter[q], total[q], q) for q in counter]:
        if (name, val) not in waited:
            g.wait_ge(sem, val)


def rank_program(g, core, T, topo):
    rank = T.rank_of(core)
    if rank is None:
        return
    A, F = AluOpType, ActivationFunctionType
    ops, touched, ndma = [], {}, [0]
    lists = {q: [] for q in "vspgyx"}

    def op(q, fn, reads, writes, kind="c", token=None):
        touch = [(x, False) for x in reads] + [(x, True) for x in writes]
        deps = {}
        for (name, a, b), wr in touch:
            for o, a2, b2, wr2 in touched.get(name, []):
                if ((name in PSUM and o["q"] != q) or ((wr or wr2) and a < b2 and a2 < b)) and not (o["q"] == "p" and q == "p"):
                    deps[o["n"]] = o
        if kind == "d":
            token = (T.sem["d%d" % ndma[0]], 16, "d%d" % ndma[0])
            ndma[0] += 1
        o = {"q": q, "fn": fn, "w": writes, "kind": kind, "tok": token, "deps": [deps[n] for n in sorted(deps)], "n": len(ops)}
        ops.append(o)
        for (name, a, b), wr in touch:
            touched.setdefault(name, []).append((o, a, b, wr))
        return o

    def put(*some):
        for o in some:
            lists[o["q"]].append(o)

    def dma(q, out, src, reads, writes, add=False):
        fn = (lambda e: e.dma_start(out, src, accum_op=A.add)) if add else (lambda e: e.dma_start(out, src))
        return op(q, fn, reads, writes, "d")

    def affine(q, out, src, scale, shift, reads, writes):
        if q == "v":
            return op(q, lambda e: e.tensor_scalar(out, src, scale, shift, A.mult, A.add), reads, writes)
        return op(q, lambda e: e.activation(out, src, F.Identity, bias=shift, scale=scale), reads, writes)

    def pair(out, x, y, how, reads, writes):
        return op("v", lambda e: e.tensor_tensor(out, x, y, how), reads, writes)

    def fill(name, a, b, val, step=1):
        return op("v", lambda e: e.memset(T[name][:, a:b:step] if step > 1 else T[name][:, a:b], val), [], [(name, a, b)])

    def pick(out, src, a, b, pattern, cmp, base, cm):
        return op("g", lambda e: e.affine_select(T[out][:, a:b], T[src][:, a:b], pattern, cmp, 0.0, base, cm), [(src, a, b)], [(out, a, b)])

    def cast(out, src, a, b):
        return pick(out, src, a, b, [[0, b - a]], A.is_ge, 0, 0)

    start = [sum(BANKS[:k]) for k in range(NB)]
    banks = [(k, start[k], start[k] + BANKS[k]) for k in range(NB)]
    dsts = [T.cores[(rank + d) % N] for d in range(1, N)]
    order, calls = calls_of(topo, T.cores, rank)
    landing = 0
    for d in range(1, N):
        q = (rank - d) % N
        for js, _, _ in calls_of(topo, T.cores, q)[1]:
            landing += len(engine_plan(topo, T.cores[q], [T.cores[(q + 1 + j) % N] for j in js], T.cores).get(core, []))
    place, n = {}, 0
    for js, a, b in calls:
        for j in sorted(js):
            place[j, a] = n
            n += b - a

    def R(k, a, b):
        return T["R%d" % k][:, a - start[k]:b - start[k]]

    def bank(k):
        return ("R%d" % k, 0, 512)

    def into(k, eye, src, shift, a, b, begin, end):
        return op("p", lambda e: e.matmul(R(k, a, b), T.eye[:, eye:eye + 128], T[src][:, shift + a:shift + b], begin, end),
                  [("eye", 0, 256), (src, shift + a, shift + b)], [bank(k)])

    def thresholds(t, k, a, b):
        if t == 0:
            r, rr, y, yy = T.r0i[:, a:b], ("r0i", a, b), T[STAGE[k]][:, 0:b - a], (STAGE[k], 0, 512)
        else:
            r, rr, y, yy = R(k, a, b), bank(k), T.Y[:, a:b], ("Y", a, b)
        return [op("s", lambda e: e.activation(y, r, F.Relu, bias=T.bias[:, 0:1], scale=BIG), [rr, ("bias", 0, 1)], [yy]),
                pair(T["ro%d" % t][:, Z + a:Z + b], r, y, A.min, [rr, yy], [("ro%d" % t, Z + a, Z + b)])]

    put(dma("s", T.thi[:, 0:1], T.th[:], [], [("thi", 0, 4)]), dma("s", T.sni[:], T.snd[:], [], [("sni", 0, 96)]))
    loads = list(zip(LOADS[:-1], LOADS[1:]))
    for a, b in loads:
        put(dma("y", T.r0i[:, a:b], T.r0[:, a:b], [], [("r0i", a, b)]))
    put(dma("y", T.nbi[:], T.nb[:], [("r0i", V - 1, V)], [("nbi", 0, 512)]))
    put(fill("eye0", 0, 128, 1.0), fill("eye0", 128, 256, -1.0), fill("t1", 0, 144, 0.0), fill("ck", 0, 128, -K), fill("t1", 15, 144, 1.0, 16),
        fill("rst", 0, 96, -1.0e9),
        op("v", lambda e: e.tensor_scalar(T.bias[:, 0:1], T.thi[:, 0:1], -0.5, -BIG, A.add, A.mult), [("thi", 0, 4)], [("bias", 0, 1)]),
        fill("ro0", 0, Z, 0.0), fill("rst", 0, 96, CAP * K, 32),
        op("v", lambda e: e.tensor_copy(T.bias[:, 1:2], T.thi[:, 0:1]), [("thi", 0, 4)], [("bias", 1, 2)]),
        op("v", lambda e: e.tensor_copy(T.sno[:], T.sni[:]), [("sni", 0, 96)], [("sno", 0, 96)]),
        op("v", lambda e: e.tensor_copy(T.sne[:], T.sni[:, :, 0:CAP // 16]), [("sni", 0, 96)], [("sne", 0, 24)]))
    put(pick("eye", "eye0", 0, 256, [[0, 2], [-1, 128]], A.is_equal, 0, 1),
        pick("t3", "ck", 0, 128, [[-16, 8], [0, 16]], A.is_ge, 0, 1),
        pick("t2", "t1", 0, 144, [[1, 144]], A.is_ge, 0, -1),
        pick("t4", "ck", 0, 128, [[16, 8], [0, 16]], A.is_ge, 15, -1),
        cast("r0f", "r0i", banks[0][1], banks[0][2]),
        pick("bw", "t2", 0, 144, [[-1, 144]], A.is_ge, 15, 1),
        pick("lo", "t3", 0, 128, [[1, 128]], A.is_gt, 0, -1),
        pick("up", "t4", 0, 128, [[-1, 128]], A.is_ge, 0, 1))
    put(*[cast("r0f", "r0i", a, b) for _, a, b in banks[1:CAST_G]])
    held = {("v", "n8"): affine("v", T.sn8[:], T.sni[:], 1.0, float(Z), [("sni", 0, 96)], [("sn8", 0, 96)])}
    for t in range(1, RO):
        held["v", "z%d" % t] = fill("ro%d" % t, 0, Z, 0.0)
    for k, (a, b) in enumerate(loads):
        put(*thresholds(0, k, a, b))
    first_opens = [into(k, 0, "r0f", 0, a, b, True, False) for k, a, b in banks[:CAST_G]]

    def under_way(t, named):
        ro, W, sb, of, dp = ("ro%d" % t, "W%d" % t, "sb%d" % t, "of%d" % t, "dp%d" % t)
        last = t == RO - 1
        spare = {"v": [], "s": [], "p": list(first_opens) if t == 0 else [], "g": []}

        def count(n, blocks):
            s0, s1, qn = min(blocks) * G, (max(blocks) + 1) * G, "q%d" % n
            sm, c0, c1, w = s0 + FLAGS_V[t][n], s0 // 16, s1 // 16, (s1 - s0) // 16
            for q, a, b in (("v", s0, sm), ("s", sm, s1)):
                if a == b:
                    continue
                src = "Y" if t else "r0i"
                win, out = T[src][:, 0:V].indirect(T.sno[:, a // 16:b // 16]), T.fl[:, a:b]
                rd, wr = [(src, 0, V), ("sno", 0, 96)], [("fl", a, b)]
                if t:
                    o = affine(q, out, win, 1.0, 0.0, rd, wr)
                elif q == "s":
                    o = op(q, lambda e, out=out, win=win: e.activation(out, win, F.Relu, bias=T.bias[:, 0:1], scale=BIG), rd + [("bias", 0, 4)], wr)
                else:
                    o = op(q, lambda e, out=out, win=win: e.tensor_scalar(out, win, T.bias[:, 1:2], None, A.is_ge), rd + [("bias", 0, 4)], wr)
                named[q, "f%d" % n] = o
            step = 8 if t and w == 32 else 16
            hot, h0, hw = ("hot2", 0, 64) if step == 8 else ("hot", c0, w)

            def seeds(e):
                for i in range(step):
                    ins = e.matmul(T[qn][:, 0:hw], T.bw[:, 15 - i:143 - i], T.fl[:, s0 + i:s1:step], i == 0, i == step - 1)
                return ins

            def before(e):
                if step == 8:
                    runs = [(128, "lo", T.hot2[:, 0:64:2], 32), (128, "lo8", T.hot2[:, 1:64:2], 32),
                            (129, "up", T.hot2[:, 0:62:2], 31), (129, "up8", T.hot2[:, 1:62:2], 31)]
                else:
                    runs = [(128, "lo", T.hot[:, c0:c1], w)] + [(129 + x, "up", T.hot[:, c0 + x:c0 + x + 31], 31) for x in range(0, w, 32)]
                for i, (x, tri, rhs, m) in enumerate(runs):
                    ins = e.matmul(T[qn][:, x:x + m], T[tri][:], rhs, i == 0, i == len(runs) - 1)
                return ins

            tris = [(x, 0, 128) for x in (("lo", "up", "lo8", "up8") if step == 8 else ("lo", "up"))]
            named["p", "s%d" % n] = op("p", seeds, [("bw", 0, 144), ("fl", s0, s1)], [(qn, 0, hw)])
            named["v", "h%d" % n] = op("v", lambda e: e.tensor_scalar(T[hot][:, h0:h0 + hw], T[qn][:, 0:hw], 1.0, None, A.min),
                                       [(qn, 0, hw)], [(hot, h0, h0 + hw)])
            named["p", "t%d" % n] = op("p", before, tris + [(hot, h0, h0 + hw)], [(qn, 128, 128 + w)])
            named["v", "c%d" % n] = op("v", lambda e: e.tensor_tensor_scan(T.cnt[:, c0:c1], T.rst[:, c0:c1], T[qn][:, 128:128 + w], 0.0, A.max, A.add),
                                       [("rst", 0, 96), (qn, 128, 128 + w)], [("cnt", c0, c1)])
            named["v", "o%d" % n] = pair(T[of][:, c0:c1], T.cnt[:, c0:c1], T.sn8[:, c0:c1], A.min, [("cnt", c0, c1), ("sn8", 0, 96)], [(of, c0, c1)])

        def values(name, tile, base, col, a, b, nv):
            for q, x, y in (("v", a, a + nv), ("s", a + nv, b)):
                if x < y:
                    c0, c1 = col + (x - a) // 16, col + (y - a) // 16
                    named[q, name] = affine(q, T[sb][:, x:y], T[ro][:, base:Z + V].indirect(T[tile][:, c0:c1]), EIGHTH, DOWN,
                                            [(ro, 0, Z + V), (tile, c0, c1)], [(sb, x, y)])

        def send(n):
            js, a, b = calls[n]
            name = "snt%d" % (len(calls) * t + n)
            plan = engine_plan(topo, core, [dsts[j] for j in js], T.cores)
            trs = []
            for j in js:
                rid, pid, _ = topo.addr(dsts[j])
                trs.append(RemoteDMATransfer(dst_ids=[DstId(rid=rid, pnc=pid)], dma_engine_mask=sum(1 << x for x in plan[dsts[j]]),
                                             remote_sem=T.sem["arr%d" % t], src=T[sb][:, place[j, a]:place[j, a] + b - a],
                                             dst=T[W][:, V + j * G + a:V + j * G + b]))
            return op("g", lambda e: e.remote_dma_fused(trs, local_sem=T.sem[name]), [(sb, place[j, a], place[j, a] + b - a) for j in js], [], "r",
                      (T.sem[name], sum(len(plan[dsts[j]]) for j in js), name))

        for n, part in enumerate(COUNTS):
            count(n, [order[i] for i in part])
        values("e", "sne", Z, 0, 0, (N - 1) * CAP, (N - 1) * CAP)
        for i, j in enumerate(order):
            values("v%d" % i, of, 0, (j * G + CAP) // 16, place[j, CAP], place[j, CAP] + G - CAP, LATE_V[i])
        sends = [send(n) for n in range(len(calls))]
        for n, o in enumerate(sends):
            named["g", "x%d" % n] = o
        put(op("x", None, [], [(W, V, WN)], "x", (T.sem["arr%d" % t], landing, "arr%d" % t)))

        for k, a, b in banks:
            if t == 0 and k < CAST_G:
                spare["p"].append(into(k, 128, ro, Z, a, b, False, False))
                continue
            w = FL if t == 0 or k == 0 else 512
            for x in range(a, b, w):
                y = min(b, x + w)
                r, rr = (R(k, x, y), bank(k)) if t else (T.r0i[:, x:y], ("r0i", x, y))
                spare["v"].append(pair(T.r0f[:, x:y], r, T[ro][:, Z + x:Z + y], A.subtract, [rr, (ro, Z + x, Z + y)], [("r0f", x, y)]))
            if k < NB - 1:
                spare["p"].append(into(k, 0, "r0f", 0, a, b, True, False))
        if t == 0:
            named["g", "l8"] = pick("lo8", "t3", 0, 128, [[1, 128]], A.is_gt, -8, -1)
            named["g", "u8"] = pick("up8", "t4", 0, 128, [[-1, 128]], A.is_ge, 8, 1)
            named["g", "nb"] = cast("nbo", "nbi", 0, 512)
        cuts = list(range(0, FL * S_SHORT[t] + 1, FL)) + [V - S_V[t], V]
        for a, b in zip(cuts[:-1], cuts[1:]):
            q = "v" if b == V else "s"
            spare[q].append(affine(q, T[W][:, a:b], T[ro][:, Z + a:Z + b], EIGHTH, DOWN, [(ro, Z + a, Z + b)], [(W, a, b)]))
        for a in range(0, V, 512):
            b, qn = a + 512, "q%d" % (a // 512 % 3)
            if last:
                spare["s"].append(affine("s", T[qn][:], T[W][:, a:b], -4.0, 0.0, [(W, a, b)], [(qn, 0, 512)]))
                spare["v"].append(pair(T[dp][:, a:b], T[qn][:], T[ro][:, Z + a:Z + b], A.add, [(qn, 0, 512), (ro, Z + a, Z + b)], [(dp, a, b)]))
            else:
                q = "v" if b == V else "s"
                spare[q].append(affine(q, T[dp][:, a:b], T[W][:, a:b], -4.0, 0.0, [(W, a, b)], [(dp, a, b)]))
        if not last:
            o = dma("g" if t else "y", T.yp[:], T[ro][:, Z:Z + V], [(ro, Z, Z + V)], [("yp", 0, V)], t > 0)
            o["deps"].append(sends[-1])
            if t:
                named["g", "ro"] = o
            else:
                put(o)
        for n, (a, b) in enumerate([(V // 2, V), (0, V // 2)] if last else [(0, V)]):
            named["g", "p%d" % n] = dma("g", T.yp[:, a:b], T[dp][:, a:b], [(dp, a, b), (W, V, WN)], [("yp", a, b)], True)
        for q in ORDER:
            for name in ORDER[q][t].split():
                put(spare[q].pop(0) if name == "+" else named.pop((q, name)))
            put(*spare[q])

    def sums(t):
        W, last = "W%d" % t, t == RO - 1

        def gather(out, a, b, i, plus=None):
            win, rd = T[W][:, 0:WN].indirect(T.nbo[:, i * 128 + a // 16:i * 128 + b // 16]), [(W, 0, WN), ("nbo", 0, 512)]
            if plus is None:
                return op("s", lambda e: e.activation(T[out][:, a:b], win, F.Copy), rd, [(out, a, b)])
            return pair(T[out][:, a:b], win, T[plus][:, a:b], A.add, rd + [(plus, a, b)], [(out, a, b)])

        def close(k):
            _, x, y = banks[k]
            out, wr = (T.r0f[:, x:y], ("r0f", x, y)) if last else (R(k, x, y), bank(k))
            some = []
            if k in ADD_V[t]:
                some.append(pair(out, R(k, x, y), T.ac1[:, x:y], A.add, [bank(k), ("ac1", x, y)], [wr]))
            elif last:
                some.append(affine("s", out, R(k, x, y), 1.0, 0.0, [bank(k)], [wr]))
            if last:
                return some + [dma("s" if k == NB - 1 else "y", T.yr[:, x:y], out, [wr], [("yr", x, y)])]
            return some + thresholds(t + 1, k, x, y)

        k, x, y = banks[NB - 1]
        put(gather("ac0", x, y, 0, "r0f"), gather("pc1", x, y, 1, "ac0"), into(k, 0, "pc1", 0, x, y, True, False))
        after = []
        for a, b in zip(CHUNKS[:-1], CHUNKS[1:]):
            k = max(j for j in range(NB) if start[j] <= a)
            if last and b == x:
                put(*after[:4])
                del after[:4]
            pieces, closing = 1 if k in ADD_V[t] else 2, b == start[k] + BANKS[k]
            put(gather("pc0", a, b, 2), gather("pc1", a, b, 3))
            for i in range(2):
                put(gather("ac%d" % i, a, b, i, "pc%d" % i))
                if i < pieces:
                    put(into(k, 0, "ac%d" % i, 0, a, b, False, closing and i == pieces - 1))
            if closing:
                after += close(k)
        k = NB - 1
        put(gather("pc0", x, y, 2), into(k, 0, "pc0", 0, x, y, False, False), gather("ac1", x, y, 3), into(k, 0, "ac1", 0, x, y, False, True))
        after += close(k)
        if last:
            put(*after)
            return {}
        adds = [o for o in after if o["w"][0][0] in PSUM]
        rest = [o for o in after if o["w"][0][0] not in PSUM]
        put(*(adds + rest[:-4]))
        return {("s", "Y3"): rest[-4], ("v", "ro3"): rest[-3], ("s", "Y4"): rest[-2], ("v", "ro4"): rest[-1]}

    for t in range(RO):
        under_way(t, held)
        held = sums(t)
    issue(g, T, ops, lists)
